import numpy as np
import ml_dtypes


def mxq(x, axis, fmt="e4m3"):
    dtype, down = {"e4m3": (ml_dtypes.float8_e4m3fn, 7), "e5m2": (ml_dtypes.float8_e5m2, 14)}[fmt]
    v = np.moveaxis(np.asarray(x, np.float32).astype(ml_dtypes.bfloat16).astype(np.float64), axis, -1)
    blocks = v.reshape(v.shape[:-1] + (-1, 32))
    amax = np.abs(blocks).max(-1, keepdims=True)
    byte = np.maximum(np.where(amax > 0, np.frexp(amax)[1] - 1 + 127, 0) - down, 1)
    scale = np.exp2(byte - 127.0)
    codes = (blocks / scale).astype(np.float32).astype(dtype).astype(np.float64)
    return np.moveaxis((codes * scale).reshape(v.shape), -1, axis)


WIDE = False


def mx_kscale(k):
    if not WIDE:
        return np.ones(k)
    levels = np.array([10, -10, 5, -5, 0])
    if k % 512:
        return np.exp2(np.random.permutation(np.resize(levels, k // 32))).repeat(32)
    a = np.empty((k // 512, 16))
    for p in range(k // 512):
        a[p, :8] = np.random.permutation(np.resize(levels, 8))
        for g in range(8):
            far = levels[np.abs(levels - a[p, g]) >= 10]
            a[p, g + 8] = far[np.random.randint(len(far))]
    return np.exp2(a.ravel()).repeat(32)


def f64(x):
    return np.asarray(x).astype(np.float64)


def striped(idx):
    return np.tile(idx.reshape(-1, 16).T, (8, 1)).astype(np.uint16)


def unstriped(offs):
    return offs[:16].T.reshape(-1).astype(np.int64)


E2M1 = np.array([0.0, 0.5, 1.0, 1.5, 2.0, 3.0, 4.0, 6.0, -0.0, -0.5, -1.0, -1.5, -2.0, -3.0, -4.0, -6.0])


def pack_weight(w, fmt):
    k, n = w.shape
    w = f64(np.asarray(w, np.float32).astype(ml_dtypes.bfloat16)).reshape(k // 32, 32, n)
    amax = np.abs(w).max(1)
    if fmt == "e4m3":
        byte = np.frexp(amax)[1] - 1 + 127 - 7
    else:
        mant, ex = np.frexp(amax / 6.0)
        byte = np.where(mant > 0.5, ex, ex - 1) + 127
    byte = np.clip(np.where(amax > 0, byte, 1), 1, 254)
    scaled = (w * np.exp2(127.0 - byte)[:, None, :]).reshape(k, n).astype(np.float32)
    by_word = np.ascontiguousarray(scaled.reshape(k // 512, 128, 4, n).transpose(0, 1, 3, 2))
    if fmt == "e4m3":
        words = by_word.astype(ml_dtypes.float8_e4m3fn).view(np.uint8)
    else:
        c = by_word.astype(ml_dtypes.float4_e2m1fn).view(np.uint8) & 0xF
        words = (c[..., 0::2] | (c[..., 1::2] << 4)).reshape(k // 512, 128, 2 * n)
    return np.ascontiguousarray(words), np.ascontiguousarray(byte.astype(np.uint8).reshape(k // 512, 16, n))


def unpack_weight(words, scales, fmt):
    g, _, n = scales.shape
    words = np.ascontiguousarray(words).reshape(g, 128, n, -1)
    if fmt == "e4m3":
        vals = words.view(ml_dtypes.float8_e4m3fn).astype(np.float64)
    else:
        nib = np.empty((g, 128, n, 4), np.uint8)
        nib[..., 0::2] = words & 0xF
        nib[..., 1::2] = words >> 4
        vals = E2M1[nib]
    vals = vals * np.repeat(np.exp2(scales.astype(np.float64) - 127.0), 8, axis=1)[..., None]
    return vals.transpose(0, 1, 3, 2).reshape(g * 512, n)


def gelu(v):
    return 0.5 * v * (1.0 + np.tanh(np.sqrt(2.0 / np.pi) * (v + 0.044715 * v**3)))


def striped8(idx):
    return np.concatenate([v.reshape(-1, 16).T for v in idx]).astype(np.uint16)


def unstriped8(offs):
    return np.stack([offs[16 * g:16 * g + 16].T.reshape(-1) for g in range(8)]).astype(np.int64)


def heads(h, wgt, idx8):
    r = np.arange(h.shape[0])
    return wgt[r // 4 % 128] * h[r[:, None], idx8[r % 512 // 64]]


def put_heads(h, wgs, idx8, t2):
    r = np.arange(h.shape[0])
    page = np.zeros((h.shape[0], t2))
    page[r[:, None], idx8[r % 512 // 64]] = wgs[r // 4 % 128] * h
    return page


K, T, S, H, T2, P, N = 1024, 4096, 1024, 1024, 2048, 1024, 384

def setup_inputs():
    n = np.random.standard_normal
    s = mx_kscale(K)[:, None]
    u = mx_kscale(H)[:, None]
    d = {}
    d["tab_words"], d["tab_scales"] = pack_weight(n((K, T)) * s, "e4m3")
    d["offs"] = striped(np.random.permutation(T)[:S])
    d["offs2"] = striped8(np.stack([np.random.permutation(T2)[:S] for _ in range(8)]))
    d["offs3"] = striped8(np.stack([np.random.permutation(T2)[:P] for _ in range(8)]))
    d["w1"] = (2.5 * n((K, H)) / K**0.5 / s).astype(np.float32)
    d["w2_words"], d["w2_scales"] = pack_weight(0.8 * n((K, H)) / K**0.5 / s * u.T, "e2m1")
    d["gain"] = (3.0 * n(H) * u[:, 0]).astype(np.float32)
    d["wgs"] = np.repeat(np.random.uniform(0.5, 2.0, (8, S)), 16, axis=0).astype(np.float32)
    d["wgt"] = np.repeat(np.random.uniform(0.5, 2.0, (8, P)), 16, axis=0).astype(np.float32)
    d["stock"] = (1.5 * n((H, P)) * u).astype(np.float32)
    d["w3"] = (n((H, N)) / H**0.5 / u).astype(np.float32)
    return d

def reference(tab_words, tab_scales, offs, offs2, offs3, w1, w2_words, w2_scales, gain, wgs, wgt, stock, w3):
    v = unpack_weight(tab_words, tab_scales, "e4m3")[:, unstriped(offs)]
    w2 = unpack_weight(w2_words, w2_scales, "e2m1")
    need = mxq(f64(w1), 0, "e4m3").T @ v
    less = w2.T @ v
    h = f64(gain)[:, None] / (1.0 + np.exp(-need)) - less
    page = put_heads(h, f64(wgs), unstriped8(offs2), T2)
    x = heads(page, f64(wgt), unstriped8(offs3))
    z = x + np.abs(x - f64(stock))
    return mxq(f64(w3), 0, "e4m3").T @ mxq(z, 0, "e4m3")

@@ -1,0 +1,374 @@
+from contextlib import ExitStack
+
+import concourse.mybir as mybir
+from concourse.masks import make_identity
+
+K, T, S, H, T2, M, N = 1024, 4096, 1024, 1024, 2048, 1024, 384
+FLOPS = 2 * (2 * K * H * S + H * N * M)
+
+F32 = mybir.dt.float32
+BF16 = mybir.dt.bfloat16
+I32 = mybir.dt.int32
+U32 = mybir.dt.uint32
+U16 = mybir.dt.uint16
+U8 = mybir.dt.uint8
+FP8X4 = mybir.dt.float8_e4m3fn_x4
+FP4X4 = mybir.dt.float4_e2m1fn_x4
+ALU = mybir.AluOpType
+ACT = mybir.ActivationFunctionType
+
+P = 128
+PACK = 4
+PASS = P * PACK
+BANK = 512
+CHUNK = 256
+QUADS = 4
+
+
+def tile_list_refill_urgency_scores_kernel(
+    tc, tab_words, tab_scales, offs, offs2, offs3, w1, w2_words, w2_scales, gain, wgs, wgt, stock, w3, out
+):
+    nc = tc.nc
+    k_passes = K // PASS
+    r_passes = H // PASS
+    slices = r_passes * PACK
+
+    with ExitStack() as ctx:
+        lists = ctx.enter_context(tc.tile_pool(name="lists", bufs=1))
+        keep = ctx.enter_context(tc.tile_pool(name="keep", bufs=1))
+        ring = ctx.enter_context(tc.tile_pool(name="ring", bufs=2))
+        psum = ctx.enter_context(tc.psum_pool(name="psum", bufs=2))
+
+        idx = lists.tile([P, S // 16], U16, name="idx")
+        idx2 = lists.tile([P, S // 16], U16, name="idx2")
+        idx3 = lists.tile([P, M // 16], U16, name="idx3")
+
+        tab_plane = keep.tile([P, T], U8, name="tab_plane", align_bytes=64)
+        nc.vector.memset(tab_plane[:].bitcast(I32), 0)
+        w2_plane_raw = keep.tile([P, k_passes * H], U8, name="w2_plane_raw", align_bytes=64)
+        nc.vector.memset(w2_plane_raw[:].bitcast(I32), 0)
+        v_plane1 = keep.tile([P, S], U8, name="v_plane1", align_bytes=64)
+        nc.vector.memset(v_plane1[:].bitcast(I32), 0)
+        pages = [keep.tile([P, T2], F32, name="page%d" % n) for n in range(2)]
+        for page in pages:
+            nc.vector.memset(page[:], 0.0)
+        ident = keep.tile([P, P], F32, name="ident")
+        make_identity(nc, ident[:])
+        warm = keep.tile([P, 2], F32, name="warm")
+        nc.vector.memset(warm[:, 0:1], 0.0)
+
+        def load_table(a):
+            words = ring.tile([P, T], I32, name="tab%d" % a, tag="big", align_bytes=64)
+            nc.sync.dma_start(words[:], tab_words[a].rearrange("p t i -> p (t i)").bitcast(I32))
+            return words
+
+        def load_rows(weight, a, cols, name):
+            width = cols.stop - cols.start
+            raw = ring.tile([P, PACK, width], F32, name=name, tag="raw")
+            nc.sync.dma_start(raw[:], weight[a * PASS : (a + 1) * PASS, cols].rearrange("(p i) c -> p i c", i=PACK))
+            return raw
+
+        def load_stock(b):
+            rows = ring.tile([P, PACK * M], F32, name="stock%d" % b, tag="big", align_bytes=64)
+            nc.sync.dma_start(rows[:], stock[b * PASS : (b + 1) * PASS, :].rearrange("(p i) m -> p (i m)", i=PACK))
+            return rows
+
+        nc.sync.dma_start(idx[:], offs)
+        tab = [load_table(0)]
+        for q in range(QUADS):
+            nc.scalar.dma_start(
+                tab_plane[32 * q : 32 * q + 8, :].bitcast(I32), tab_scales[:, 4 * q : 4 * q + 4, :].bitcast(I32)
+            )
+        nc.scalar.activation(warm[:, 1:2], warm[:, 0:1], ACT.Sigmoid)
+        w2_raw = keep.tile([P, k_passes, H // 2], I32, name="w2_raw")
+        nc.sync.dma_start(w2_raw[:], w2_words.bitcast(I32).rearrange("a p c -> p a c"))
+        w1_raw = {(0, 0): load_rows(w1, 0, slice(0, PASS), "w1_00")}
+        for q in range(QUADS):
+            nc.sync.dma_start(
+                w2_plane_raw[32 * q : 32 * q + 4, :].bitcast(I32).rearrange("r (a c) -> r a c", a=k_passes),
+                w2_scales[:, 4 * q : 4 * q + 4, :].bitcast(I32).rearrange("a r c -> r a c"),
+            )
+        v_words = [keep.tile([P, S], U32, name="v_words%d" % a, align_bytes=64) for a in range(k_passes)]
+        v_plane = keep.tile([P, S], U8, name="v_plane", align_bytes=64)
+        nc.vector.tensor_copy(v_plane[:], tab_plane[:].indirect(idx[:]))
+        nc.vector.tensor_copy(v_words[0][:], tab[0][:].bitcast(U32).indirect(idx[:]))
+        tab.append(load_table(1))
+        nc.sync.dma_start(v_plane1[0 : P - 4, :].bitcast(I32), v_plane[4:P, :].bitcast(I32))
+        w1_raw[0, 1] = load_rows(w1, 1, slice(0, PASS), "w1_01")
+        gains = keep.tile([P, r_passes, PACK], F32, name="gains")
+        nc.sync.dma_start(gains[:], gain.rearrange("(b p i) -> p b i", b=r_passes, i=PACK))
+        nc.sync.dma_start(idx2[:], offs2)
+        put_weight = keep.tile([P, S], F32, name="put_weight")
+        nc.sync.dma_start(put_weight[:], wgs)
+        nc.sync.dma_start(idx3[:], offs3)
+        read_weight = keep.tile([P, M], F32, name="read_weight")
+        nc.sync.dma_start(read_weight[:], wgt)
+        stocks = [load_stock(0)]
+
+        w2_codes = keep.tile([P, k_passes * H * 2], U8, name="w2_codes", align_bytes=64)
+        nc.vector.tensor_copy(
+            w2_codes[:].bitcast(U16).rearrange("p (g i q) -> p g i q", i=PACK, q=P),
+            w2_raw[:].rearrange("p a c -> p (a c)").bitcast(U16).rearrange("p (g q i) -> p g i q", i=PACK, q=P),
+        )
+        w2_plane = keep.tile([P, k_passes * H], U8, name="w2_plane", align_bytes=64)
+        nc.vector.tensor_copy(
+            w2_plane[:].rearrange("p (g i q) -> p g i q", i=PACK, q=P),
+            w2_plane_raw[:].rearrange("p (g q i) -> p g i q", i=PACK, q=P),
+        )
+
+        w1_codes = {}
+        w1_plane = {}
+
+        def quantise_w1(b, a, parts):
+            codes = keep.tile([P, PASS], U32, name="w1_codes%d%d" % (b, a), align_bytes=64)
+            plane = keep.tile([P, PASS], U8, name="w1_plane%d%d" % (b, a), align_bytes=64)
+            w1_codes[b, a], w1_plane[b, a] = codes, plane
+            rounded = []
+            for first, count, copy in parts:
+                part = ring.tile([P, count * PASS], BF16, name="w1_bf", tag="w1_bf", bufs=3, align_bytes=64)
+                copy(
+                    part[:].rearrange("p (i q j) -> p q i j", i=count, j=PACK),
+                    w1_raw[b, a][:].rearrange("p j (q i) -> p q i j", i=PACK)[:, :, first : first + count, :],
+                )
+                rounded.append(part)
+            for (first, count, copy), part in zip(parts, rounded):
+                cols = slice(first * P, (first + count) * P)
+                nc.vector.quantize_mx(out=codes[:, cols].bitcast(FP8X4), scales=plane[:, cols], in_=part[:])
+
+        quantise_w1(0, 0, [(0, PACK, nc.scalar.copy)])
+        nc.vector.tensor_copy(v_words[1][:], tab[1][:].bitcast(U32).indirect(idx[:]))
+        quantise_w1(0, 1, [(0, 1, nc.vector.tensor_copy), (1, 2, nc.scalar.copy), (3, 1, nc.vector.tensor_copy)])
+
+        def put(n, h, first, width):
+            cols = slice(first, first + width)
+            nc.vector.tensor_tensor(
+                pages[n % 2][:].indirect(idx2[:, first // 16 : (first + width) // 16]),
+                h[:, cols],
+                put_weight[:, cols],
+                ALU.mult,
+            )
+
+        def features(n):
+            b, i = divmod(n, PACK)
+            h = ring.tile([P, S], F32, name="h", tag="h", bufs=3)
+            for half in range(S // BANK):
+                cols = slice(half * BANK, (half + 1) * BANK)
+                need = psum.tile([P, BANK], F32, name="need", tag="need")
+                less = psum.tile([P, BANK], F32, name="less", tag="less")
+                for a in range(k_passes):
+                    nc.tensor.matmul_mx(
+                        out=need[:],
+                        lhsT=w1_codes[b, a][:, i * P : (i + 1) * P].bitcast(FP8X4),
+                        lhsT_scale=w1_plane[b, a][:, i * P : (i + 1) * P],
+                        rhs=v_words[a][:, cols].bitcast(FP8X4),
+                        rhs_scale=v_plane[4 * a : P, cols],
+                        start=(a == 0),
+                        stop=(a == k_passes - 1),
+                    )
+                for a in range(k_passes):
+                    first = a * H + n * P
+                    nc.tensor.matmul_mx(
+                        out=less[:],
+                        lhsT=w2_codes[:, 2 * first : 2 * (first + P)].bitcast(FP4X4),
+                        lhsT_scale=w2_plane[:, first : first + P],
+                        rhs=v_words[a][:, cols].bitcast(FP8X4),
+                        rhs_scale=[v_plane, v_plane1][a][:, cols],
+                        start=(a == 0),
+                        stop=(a == k_passes - 1),
+                    )
+                gate = ring.tile([P, BANK], F32, name="gate", tag="gate", bufs=3)
+                nc.scalar.activation(gate[:], need[:], ACT.Sigmoid)
+                nc.vector.scalar_tensor_tensor(
+                    h[:, cols], gate[:], gains[:, b, i : i + 1], less[:], ALU.mult, ALU.subtract
+                )
+                if n == 0:
+                    put(n, h, half * BANK, BANK)
+            return h
+
+        def read(n, minus_x, first, width):
+            cols = slice(first, first + width)
+            nc.vector.tensor_tensor(
+                minus_x[:, cols],
+                pages[n % 2][:].indirect(idx3[:, first // 16 : (first + width) // 16]),
+                read_weight[:, cols],
+                ALU.mult,
+            )
+
+        def add_turned(bank, block, tiles, col):
+            for pos, source in enumerate(tiles):
+                nc.tensor.matmul(
+                    bank[:, block * P : (block + 1) * P],
+                    lhsT=source[:, col : col + P],
+                    rhs=ident[:],
+                    is_transpose=True,
+                    start=(pos == 0),
+                    stop=(pos == len(tiles) - 1),
+                )
+
+        stock_turned = {}
+        excess_turned = {}
+
+        def stock_rows(n):
+            b, i = divmod(n, PACK)
+            return stocks[b][:, i * M : (i + 1) * M]
+
+        def turn_stock(n):
+            turned = ring.tile([P, M], F32, name="stock_turned", tag="stock_turned", bufs=3)
+            for half in range(M // BANK):
+                bank = psum.tile([P, BANK], F32, name="bank", tag="work", bufs=4)
+                for block in range(BANK // P):
+                    add_turned(bank, block, [stock_rows(n)], half * BANK + block * P)
+                nc.scalar.copy(turned[:, half * BANK : (half + 1) * BANK], bank[:])
+            stock_turned[n] = turned
+
+        def excess(n, minus_x):
+            turned = ring.tile([P, M], F32, name="excess_turned", tag="excess_turned", bufs=3)
+            for half in range(M // BANK):
+                bank = psum.tile([P, BANK], F32, name="bank", tag="work", bufs=4)
+                for block in range(BANK // P):
+                    add_turned(bank, block, [stock_rows(n), minus_x], half * BANK + block * P)
+                nc.scalar.activation(turned[:, half * BANK : (half + 1) * BANK], bank[:], ACT.Relu, scale=-2.0)
+            excess_turned[n] = turned
+
+        z_bf = {}
+
+        def z_tile(b, c):
+            if (b, c) not in z_bf:
+                z_bf[b, c] = ring.tile([P, CHUNK, PACK], BF16, name="z_bf", tag="z_bf", bufs=4, align_bytes=64)
+            return z_bf[b, c]
+
+        def z_pair(n):
+            b, i = divmod(n, PACK)
+            for c in range(M // CHUNK):
+                bank = psum.tile([P, BANK], F32, name="bank", tag="work", bufs=4)
+                for side in range(2):
+                    for block in range(CHUNK // P):
+                        add_turned(
+                            bank,
+                            side * (CHUNK // P) + block,
+                            [stock_turned[n + side], excess_turned[n + side]],
+                            c * CHUNK + block * P,
+                        )
+                nc.scalar.copy(z_tile(b, c)[:, :, i : i + 2], bank[:].rearrange("p (s m) -> p m s", s=2))
+
+        z_codes = [keep.tile([P, M], U32, name="z_codes%d" % b, align_bytes=64) for b in range(r_passes)]
+        z_plane = [keep.tile([P, M], U8, name="z_plane%d" % b, align_bytes=64) for b in range(r_passes)]
+
+        def quantise_z(b, c):
+            cols = slice(c * CHUNK, (c + 1) * CHUNK)
+            nc.vector.quantize_mx(
+                out=z_codes[b][:, cols].bitcast(FP8X4),
+                scales=z_plane[b][:, cols],
+                in_=z_tile(b, c)[:].rearrange("p m i -> p (m i)"),
+            )
+
+        w3_codes = keep.tile([P, r_passes * N], U32, name="w3_codes", align_bytes=64)
+        w3_plane = keep.tile([P, r_passes * N], U8, name="w3_plane", align_bytes=64)
+
+        def quantise_w3():
+            rounded = keep.tile([P, r_passes * N * PACK], BF16, name="w3_bf", align_bytes=64)
+            for b in range(r_passes):
+                raw = load_rows(w3, b, slice(0, N), "w3_raw")
+                nc.scalar.copy(
+                    rounded[:, b * N * PACK : (b + 1) * N * PACK].rearrange("p (c e j) -> p c j e", e=4, j=PACK),
+                    raw[:].rearrange("p j (c e) -> p c j e", e=4),
+                )
+            for first, width in ((0, 512), (512, 256)):
+                nc.vector.quantize_mx(
+                    out=w3_codes[:, first : first + width].bitcast(FP8X4),
+                    scales=w3_plane[:, first : first + width],
+                    in_=rounded[:, first * PACK : (first + width) * PACK],
+                )
+
+        score_banks = {}
+
+        def score_pass(c, b):
+            cols = slice(c * CHUNK, (c + 1) * CHUNK)
+            if b == 0:
+                score_banks[c] = [
+                    psum.tile([P, BANK], F32, name="pair_bank", tag="need"),
+                    psum.tile([P, BANK], F32, name="lone_bank", tag="less"),
+                ]
+            for tile_n in range(N // P):
+                first = b * N + tile_n * P
+                nc.tensor.matmul_mx(
+                    out=score_banks[c][tile_n // 2][:, (tile_n % 2) * CHUNK : (tile_n % 2 + 1) * CHUNK],
+                    lhsT=w3_codes[:, first : first + P].bitcast(FP8X4),
+                    lhsT_scale=w3_plane[:, first : first + P],
+                    rhs=z_codes[b][:, cols].bitcast(FP8X4),
+                    rhs_scale=z_plane[b][:, cols],
+                    start=(b == 0 and tile_n != 1),
+                    stop=(b == r_passes - 1 and tile_n != 0),
+                )
+
+        def store_scores(c, lone_copy):
+            cols = slice(c * CHUNK, (c + 1) * CHUNK)
+            pair = ring.tile([P, BANK], F32, name="staged_pair", tag="staged_pair", bufs=3)
+            nc.scalar.copy(pair[:], score_banks[c][0][:])
+            nc.sync.dma_start(
+                out[0 : 2 * P, cols].rearrange("(g p) m -> p g m", p=P), pair[:].rearrange("p (g m) -> p g m", m=CHUNK)
+            )
+            lone = ring.tile([P, CHUNK], F32, name="staged_lone", tag="staged_lone", bufs=3)
+            lone_copy(lone[:], score_banks[c][1][:, 0:CHUNK])
+            nc.sync.dma_start(out[2 * P : N, cols], lone[:])
+
+        features(0)
+        nc.scalar.mul(read_weight[:], read_weight[:], -1.0)
+        h_next = features(1)
+        last = slices - 1
+        pair_in = keep.tile([P, 2, M], F32, name="pair_in")
+        for n in range(last):
+            minus_x = ring.tile([P, M], F32, name="minus_x", tag="minus_x")
+            read(n, minus_x, 0, M)
+            put(n + 1, h_next, 0, S)
+            if n == 0:
+                for a in range(k_passes):
+                    w1_raw[1, a] = load_rows(w1, a, slice(PASS, 2 * PASS), "w1_1%d" % a)
+                    quantise_w1(1, a, [(0, PACK, nc.scalar.copy)])
+                stocks.append(load_stock(1))
+            if n + 2 < slices:
+                h_next = features(n + 2)
+            turn_stock(n)
+            excess(n, minus_x)
+            if n % 2 == 1:
+                z_pair(n - 1)
+            if n == PACK - 1:
+                for c in range(M // CHUNK):
+                    quantise_z(0, c)
+            if n == 2:
+                quantise_w3()
+            if n == last - 1:
+                for half in range(M // BANK):
+                    bank = psum.tile([P, BANK], F32, name="bank", tag="work", bufs=4)
+                    for block in range(BANK // P):
+                        add_turned(bank, block, [stock_turned[n], excess_turned[n]], half * BANK + block * P)
+                    nc.scalar.copy(pair_in[:, 0, half * BANK : (half + 1) * BANK], bank[:])
+
+        minus_x = ring.tile([P, M], F32, name="minus_x", tag="minus_x")
+        pair_stock = stocks[1][:, 2 * M : 4 * M].rearrange("p (s m) -> p m s", s=2)
+        chunks = M // CHUNK
+        score_pass(0, 0)
+        score_pass(1, 0)
+        for step in range(chunks + 3):
+            if step < chunks:
+                read(last, minus_x, step * CHUNK, CHUNK)
+            if 1 <= step <= chunks:
+                cols = slice((step - 1) * CHUNK, step * CHUNK)
+                nc.vector.scalar_tensor_tensor(
+                    pair_in[:, 1, cols], minus_x[:, cols], -2.0, stock_rows(last)[:, cols], ALU.mult, ALU.subtract
+                )
+            if 2 <= step <= chunks + 1:
+                c = step - 2
+                cols = slice(c * CHUNK, (c + 1) * CHUNK)
+                nc.vector.tensor_tensor(
+                    z_tile(1, c)[:, :, 2:4],
+                    pair_in[:].rearrange("p s m -> p m s")[:, cols, :],
+                    pair_stock[:, cols, :],
+                    ALU.max,
+                )
+            if step >= 3:
+                quantise_z(1, step - 3)
+                score_pass(step - 3, 1)
+                store_scores(step - 3, nc.vector.tensor_copy if step == chunks + 2 else nc.scalar.copy)
+                if step - 1 < chunks:
+                    score_pass(step - 1, 0)

@@ -74,27 +74,41 @@ def tile_list_refill_urgency_scores_kernel(
             return rows
 
         nc.sync.dma_start(idx[:], offs)
-        tab = [load_table(0)]
-        for q in range(QUADS):
-            nc.scalar.dma_start(
-                tab_plane[32 * q : 32 * q + 8, :].bitcast(I32), tab_scales[:, 4 * q : 4 * q + 4, :].bitcast(I32)
-            )
-        nc.scalar.activation(warm[:, 1:2], warm[:, 0:1], ACT.Sigmoid)
         w2_raw = keep.tile([P, k_passes, H // 2], I32, name="w2_raw")
         nc.sync.dma_start(w2_raw[:], w2_words.bitcast(I32).rearrange("a p c -> p a c"))
-        w1_raw = {(0, 0): load_rows(w1, 0, slice(0, PASS), "w1_00")}
+        for q in range(QUADS):
+            nc.sync.dma_start(
+                tab_plane[32 * q : 32 * q + 8, :].bitcast(I32), tab_scales[:, 4 * q : 4 * q + 4, :].bitcast(I32)
+            )
+        tab = [load_table(0)]
+        nc.scalar.activation(warm[:, 1:2], warm[:, 0:1], ACT.Sigmoid)
         for q in range(QUADS):
             nc.sync.dma_start(
                 w2_plane_raw[32 * q : 32 * q + 4, :].bitcast(I32).rearrange("r (a c) -> r a c", a=k_passes),
                 w2_scales[:, 4 * q : 4 * q + 4, :].bitcast(I32).rearrange("a r c -> r a c"),
             )
-        v_words = [keep.tile([P, S], U32, name="v_words%d" % a, align_bytes=64) for a in range(k_passes)]
+        w1_raw = {(0, a): load_rows(w1, a, slice(0, PASS), "w1_0%d" % a) for a in range(k_passes)}
+        w2_codes = keep.tile([P, k_passes * H * 2], U8, name="w2_codes", align_bytes=64)
+        nc.vector.tensor_copy(
+            w2_codes[:].bitcast(U16).rearrange("p (g i q) -> p g i q", i=PACK, q=P),
+            w2_raw[:].rearrange("p a c -> p (a c)").bitcast(U16).rearrange("p (g q i) -> p g i q", i=PACK, q=P),
+        )
+        v_words = [
+            [keep.tile([P, BANK], U32, name="v_words%d%d" % (a, half), align_bytes=64) for half in range(2)]
+            for a in range(k_passes)
+        ]
         v_plane = keep.tile([P, S], U8, name="v_plane", align_bytes=64)
+
+        def gather_words(a):
+            for half in range(2):
+                nc.vector.tensor_copy(
+                    v_words[a][half][:], tab[a][:].bitcast(U32).indirect(idx[:, half * 32 : (half + 1) * 32])
+                )
+
         nc.vector.tensor_copy(v_plane[:], tab_plane[:].indirect(idx[:]))
-        nc.vector.tensor_copy(v_words[0][:], tab[0][:].bitcast(U32).indirect(idx[:]))
+        gather_words(0)
         tab.append(load_table(1))
-        nc.sync.dma_start(v_plane1[0 : P - 4, :].bitcast(I32), v_plane[4:P, :].bitcast(I32))
-        w1_raw[0, 1] = load_rows(w1, 1, slice(0, PASS), "w1_01")
+        nc.scalar.dma_start(v_plane1[0 : P - 4, :].bitcast(I32), v_plane[4:P, :].bitcast(I32))
         gains = keep.tile([P, r_passes, PACK], F32, name="gains")
         nc.sync.dma_start(gains[:], gain.rearrange("(b p i) -> p b i", b=r_passes, i=PACK))
         nc.sync.dma_start(idx2[:], offs2)
@@ -103,13 +117,7 @@ def tile_list_refill_urgency_scores_kernel(
         nc.sync.dma_start(idx3[:], offs3)
         read_weight = keep.tile([P, M], F32, name="read_weight")
         nc.sync.dma_start(read_weight[:], wgt)
-        stocks = [load_stock(0)]
 
-        w2_codes = keep.tile([P, k_passes * H * 2], U8, name="w2_codes", align_bytes=64)
-        nc.vector.tensor_copy(
-            w2_codes[:].bitcast(U16).rearrange("p (g i q) -> p g i q", i=PACK, q=P),
-            w2_raw[:].rearrange("p a c -> p (a c)").bitcast(U16).rearrange("p (g q i) -> p g i q", i=PACK, q=P),
-        )
         w2_plane = keep.tile([P, k_passes * H], U8, name="w2_plane", align_bytes=64)
         nc.vector.tensor_copy(
             w2_plane[:].rearrange("p (g i q) -> p g i q", i=PACK, q=P),
@@ -125,7 +133,7 @@ def tile_list_refill_urgency_scores_kernel(
             w1_codes[b, a], w1_plane[b, a] = codes, plane
             rounded = []
             for first, count, copy in parts:
-                part = ring.tile([P, count * PASS], BF16, name="w1_bf", tag="w1_bf", bufs=3, align_bytes=64)
+                part = ring.tile([P, count * PASS], BF16, name="w1_bf", tag="w1_bf", bufs=2, align_bytes=64)
                 copy(
                     part[:].rearrange("p (i q j) -> p q i j", i=count, j=PACK),
                     w1_raw[b, a][:].rearrange("p j (q i) -> p q i j", i=PACK)[:, :, first : first + count, :],
@@ -135,64 +143,93 @@ def tile_list_refill_urgency_scores_kernel(
                 cols = slice(first * P, (first + count) * P)
                 nc.vector.quantize_mx(out=codes[:, cols].bitcast(FP8X4), scales=plane[:, cols], in_=part[:])
 
-        quantise_w1(0, 0, [(0, PACK, nc.scalar.copy)])
-        nc.vector.tensor_copy(v_words[1][:], tab[1][:].bitcast(U32).indirect(idx[:]))
-        quantise_w1(0, 1, [(0, 1, nc.vector.tensor_copy), (1, 2, nc.scalar.copy), (3, 1, nc.vector.tensor_copy)])
+        for a in range(k_passes):
+            quantise_w1(0, a, [(0, PACK, nc.scalar.copy)])
+        gather_words(1)
+
+        last = slices - 1
+
+        def page_of(n):
+            return pages[min(n, last - 1) % 2]
 
         def put(n, h, first, width):
             cols = slice(first, first + width)
             nc.vector.tensor_tensor(
-                pages[n % 2][:].indirect(idx2[:, first // 16 : (first + width) // 16]),
+                page_of(n)[:].indirect(idx2[:, first // 16 : (first + width) // 16]),
                 h[:, cols],
                 put_weight[:, cols],
                 ALU.mult,
             )
 
-        def features(n):
-            b, i = divmod(n, PACK)
-            h = ring.tile([P, S], F32, name="h", tag="h", bufs=3)
-            for half in range(S // BANK):
-                cols = slice(half * BANK, (half + 1) * BANK)
-                need = psum.tile([P, BANK], F32, name="need", tag="need")
-                less = psum.tile([P, BANK], F32, name="less", tag="less")
-                for a in range(k_passes):
-                    nc.tensor.matmul_mx(
-                        out=need[:],
-                        lhsT=w1_codes[b, a][:, i * P : (i + 1) * P].bitcast(FP8X4),
-                        lhsT_scale=w1_plane[b, a][:, i * P : (i + 1) * P],
-                        rhs=v_words[a][:, cols].bitcast(FP8X4),
-                        rhs_scale=v_plane[4 * a : P, cols],
-                        start=(a == 0),
-                        stop=(a == k_passes - 1),
-                    )
-                for a in range(k_passes):
-                    first = a * H + n * P
-                    nc.tensor.matmul_mx(
-                        out=less[:],
-                        lhsT=w2_codes[:, 2 * first : 2 * (first + P)].bitcast(FP4X4),
-                        lhsT_scale=w2_plane[:, first : first + P],
-                        rhs=v_words[a][:, cols].bitcast(FP8X4),
-                        rhs_scale=[v_plane, v_plane1][a][:, cols],
-                        start=(a == 0),
-                        stop=(a == k_passes - 1),
-                    )
-                gate = ring.tile([P, BANK], F32, name="gate", tag="gate", bufs=3)
-                nc.scalar.activation(gate[:], need[:], ACT.Sigmoid)
-                nc.vector.scalar_tensor_tensor(
-                    h[:, cols], gate[:], gains[:, b, i : i + 1], less[:], ALU.mult, ALU.subtract
-                )
-                if n == 0:
-                    put(n, h, half * BANK, BANK)
-            return h
-
-        def read(n, minus_x, first, width):
+        def read(n, x, first, width):
             cols = slice(first, first + width)
             nc.vector.tensor_tensor(
-                minus_x[:, cols],
-                pages[n % 2][:].indirect(idx3[:, first // 16 : (first + width) // 16]),
+                x[:, cols],
+                page_of(n)[:].indirect(idx3[:, first // 16 : (first + width) // 16]),
                 read_weight[:, cols],
                 ALU.mult,
             )
+
+        hs = {}
+        weighed = {}
+
+        def products(n, half):
+            b, i = divmod(n, PACK)
+            cols = slice(half * BANK, (half + 1) * BANK)
+            need = psum.tile([P, BANK], F32, name="need", tag="need")
+            less = psum.tile([P, BANK], F32, name="less", tag="less")
+            for a in range(k_passes):
+                nc.tensor.matmul_mx(
+                    out=need[:],
+                    lhsT=w1_codes[b, a][:, i * P : (i + 1) * P].bitcast(FP8X4),
+                    lhsT_scale=w1_plane[b, a][:, i * P : (i + 1) * P],
+                    rhs=v_words[a][half][:].bitcast(FP8X4),
+                    rhs_scale=v_plane[4 * a : P, cols],
+                    start=(a == 0),
+                    stop=(a == k_passes - 1),
+                )
+            for a in range(k_passes):
+                first = a * H + n * P
+                nc.tensor.matmul_mx(
+                    out=less[:],
+                    lhsT=w2_codes[:, 2 * first : 2 * (first + P)].bitcast(FP4X4),
+                    lhsT_scale=w2_plane[:, first : first + P],
+                    rhs=v_words[a][half][:].bitcast(FP8X4),
+                    rhs_scale=[v_plane, v_plane1][a][:, cols],
+                    start=(a == 0),
+                    stop=(a == k_passes - 1),
+                )
+            return need, less
+
+        def features_fused(n, half):
+            b, i = divmod(n, PACK)
+            cols = slice(half * BANK, (half + 1) * BANK)
+            if half == 0:
+                hs[n] = ring.tile([P, S], F32, name="h", tag="weighed", bufs=3)
+            need, less = products(n, half)
+            gate = ring.tile([P, BANK], F32, name="gate", tag="gate_half", bufs=2)
+            nc.scalar.activation(gate[:], need[:], ACT.Sigmoid)
+            nc.vector.scalar_tensor_tensor(
+                hs[n][:, cols], gate[:], gains[:, b, i : i + 1], less[:], ALU.mult, ALU.subtract
+            )
+
+        def features(n):
+            b, i = divmod(n, PACK)
+            gate = ring.tile([P, S], F32, name="gate", tag="gate")
+            linear = ring.tile([P, S], F32, name="linear", tag="linear")
+            for half in range(2):
+                cols = slice(half * BANK, (half + 1) * BANK)
+                need, less = products(n, half)
+                nc.scalar.activation(gate[:, cols], need[:], ACT.Sigmoid)
+                nc.scalar.copy(linear[:, cols], less[:])
+            nc.scalar.activation(gate[:], gate[:], ACT.Copy, scale=gains[:, b, i : i + 1])
+            h = ring.tile([P, S], F32, name="h", tag="hx%d" % (n % 2), bufs=1)
+            nc.gpsimd.tensor_tensor(h[:], gate[:], linear[:], ALU.subtract)
+            weighed[n] = ring.tile([P, S], F32, name="weighed", tag="weighed", bufs=3)
+            nc.gpsimd.tensor_tensor(weighed[n][:], h[:], put_weight[:], ALU.mult)
+
+        def put_weighed(n):
+            nc.vector.tensor_copy(page_of(n)[:].indirect(idx2[:]), weighed[n][:])
 
         def add_turned(bank, block, tiles, col):
             for pos, source in enumerate(tiles):
@@ -205,30 +242,30 @@ def tile_list_refill_urgency_scores_kernel(
                     stop=(pos == len(tiles) - 1),
                 )
 
-        stock_turned = {}
-        excess_turned = {}
+        z_turned = {}
 
         def stock_rows(n):
             b, i = divmod(n, PACK)
             return stocks[b][:, i * M : (i + 1) * M]
 
-        def turn_stock(n):
-            turned = ring.tile([P, M], F32, name="stock_turned", tag="stock_turned", bufs=3)
-            for half in range(M // BANK):
-                bank = psum.tile([P, BANK], F32, name="bank", tag="work", bufs=4)
-                for block in range(BANK // P):
-                    add_turned(bank, block, [stock_rows(n)], half * BANK + block * P)
-                nc.scalar.copy(turned[:, half * BANK : (half + 1) * BANK], bank[:])
-            stock_turned[n] = turned
+        def excess(n, picked, parts):
+            over = ring.tile([P, M], F32, name="over", tag="hx%d" % ((n + 1) % 2), bufs=1)
+            width = M // parts
+            for part in range(parts):
+                cols = slice(part * width, (part + 1) * width)
+                nc.gpsimd.tensor_tensor(over[:, cols], picked[:, cols], read_weight[:, cols], ALU.mult)
+                nc.gpsimd.tensor_tensor(over[:, cols], over[:, cols], stock_rows(n)[:, cols], ALU.subtract)
+                nc.scalar.activation(over[:, cols], over[:, cols], ACT.Relu, scale=2.0)
+            return over
 
-        def excess(n, minus_x):
-            turned = ring.tile([P, M], F32, name="excess_turned", tag="excess_turned", bufs=3)
+        def turn_z(n, over):
+            turned = ring.tile([P, M], F32, name="z_turned", tag="z_turned", bufs=3)
             for half in range(M // BANK):
                 bank = psum.tile([P, BANK], F32, name="bank", tag="work", bufs=4)
                 for block in range(BANK // P):
-                    add_turned(bank, block, [stock_rows(n), minus_x], half * BANK + block * P)
-                nc.scalar.activation(turned[:, half * BANK : (half + 1) * BANK], bank[:], ACT.Relu, scale=-2.0)
-            excess_turned[n] = turned
+                    add_turned(bank, block, [stock_rows(n), over], half * BANK + block * P)
+                nc.scalar.copy(turned[:, half * BANK : (half + 1) * BANK], bank[:])
+            z_turned[n] = turned
 
         z_bf = {}
 
@@ -243,12 +280,7 @@ def tile_list_refill_urgency_scores_kernel(
                 bank = psum.tile([P, BANK], F32, name="bank", tag="work", bufs=4)
                 for side in range(2):
                     for block in range(CHUNK // P):
-                        add_turned(
-                            bank,
-                            side * (CHUNK // P) + block,
-                            [stock_turned[n + side], excess_turned[n + side]],
-                            c * CHUNK + block * P,
-                        )
+                        add_turned(bank, side * (CHUNK // P) + block, [z_turned[n + side]], c * CHUNK + block * P)
                 nc.scalar.copy(z_tile(b, c)[:, :, i : i + 2], bank[:].rearrange("p (s m) -> p m s", s=2))
 
         z_codes = [keep.tile([P, M], U32, name="z_codes%d" % b, align_bytes=64) for b in range(r_passes)]
@@ -312,24 +344,37 @@ def tile_list_refill_urgency_scores_kernel(
             lone_copy(lone[:], score_banks[c][1][:, 0:CHUNK])
             nc.sync.dma_start(out[2 * P : N, cols], lone[:])
 
-        features(0)
-        nc.scalar.mul(read_weight[:], read_weight[:], -1.0)
-        h_next = features(1)
-        last = slices - 1
+        stocks = [load_stock(0)]
+        for a in range(k_passes):
+            w1_raw[1, a] = load_rows(w1, a, slice(PASS, 2 * PASS), "w1_1%d" % a)
+        stocks.append(load_stock(1))
+        for half in range(2):
+            features_fused(0, half)
+            put(0, hs[0], half * BANK, BANK)
+        for half in range(2):
+            features_fused(1, half)
+        features(2)
         pair_in = keep.tile([P, 2, M], F32, name="pair_in")
         for n in range(last):
-            minus_x = ring.tile([P, M], F32, name="minus_x", tag="minus_x")
-            read(n, minus_x, 0, M)
-            put(n + 1, h_next, 0, S)
+            picked = ring.tile([P, M], F32, name="picked", tag="picked")
+            nc.vector.tensor_copy(picked[:], page_of(n)[:].indirect(idx3[:]))
             if n == 0:
+                put(1, hs[1], 0, S)
                 for a in range(k_passes):
-                    w1_raw[1, a] = load_rows(w1, a, slice(PASS, 2 * PASS), "w1_1%d" % a)
                     quantise_w1(1, a, [(0, PACK, nc.scalar.copy)])
-                stocks.append(load_stock(1))
-            if n + 2 < slices:
-                h_next = features(n + 2)
-            turn_stock(n)
-            excess(n, minus_x)
+            else:
+                put_weighed(n + 1)
+            if n + 3 < slices and False:
+                features(n + 3)
+            over = excess(n, picked, 2 if n == last - 1 else 1)
+            if n + 3 < slices and True:
+                features(n + 3)
+            if n == last - 1:
+                for half in range(M // BANK):
+                    cols = slice(half * BANK, (half + 1) * BANK)
+                    nc.gpsimd.tensor_tensor(pair_in[:, 0, cols], over[:, cols], stock_rows(n)[:, cols], ALU.add)
+            else:
+                turn_z(n, over)
             if n % 2 == 1:
                 z_pair(n - 1)
             if n == PACK - 1:
@@ -337,25 +382,19 @@ def tile_list_refill_urgency_scores_kernel(
                     quantise_z(0, c)
             if n == 2:
                 quantise_w3()
-            if n == last - 1:
-                for half in range(M // BANK):
-                    bank = psum.tile([P, BANK], F32, name="bank", tag="work", bufs=4)
-                    for block in range(BANK // P):
-                        add_turned(bank, block, [stock_turned[n], excess_turned[n]], half * BANK + block * P)
-                    nc.scalar.copy(pair_in[:, 0, half * BANK : (half + 1) * BANK], bank[:])
 
-        minus_x = ring.tile([P, M], F32, name="minus_x", tag="minus_x")
+        x_last = ring.tile([P, M], F32, name="x_last", tag="picked")
         pair_stock = stocks[1][:, 2 * M : 4 * M].rearrange("p (s m) -> p m s", s=2)
         chunks = M // CHUNK
         score_pass(0, 0)
         score_pass(1, 0)
         for step in range(chunks + 3):
             if step < chunks:
-                read(last, minus_x, step * CHUNK, CHUNK)
+                read(last, x_last, step * CHUNK, CHUNK)
             if 1 <= step <= chunks:
                 cols = slice((step - 1) * CHUNK, step * CHUNK)
                 nc.vector.scalar_tensor_tensor(
-                    pair_in[:, 1, cols], minus_x[:, cols], -2.0, stock_rows(last)[:, cols], ALU.mult, ALU.subtract
+                    pair_in[:, 1, cols], x_last[:, cols], 2.0, stock_rows(last)[:, cols], ALU.mult, ALU.subtract
                 )
             if 2 <= step <= chunks + 1:
                 c = step - 2

@@ -49,7 +49,7 @@ def tile_list_refill_urgency_scores_kernel(
         nc.vector.memset(w2_plane_raw[:].bitcast(I32), 0)
         v_plane1 = keep.tile([P, S], U8, name="v_plane1", align_bytes=64)
         nc.vector.memset(v_plane1[:].bitcast(I32), 0)
-        pages = [keep.tile([P, T2], F32, name="page%d" % n) for n in range(2)]
+        pages = [keep.tile([P, T2], F32, name="page%d" % n) for n in range(1)]
         for page in pages:
             nc.vector.memset(page[:], 0.0)
         ident = keep.tile([P, P], F32, name="ident")
@@ -150,16 +150,7 @@ def tile_list_refill_urgency_scores_kernel(
         last = slices - 1
 
         def page_of(n):
-            return pages[min(n, last - 1) % 2]
-
-        def put(n, h, first, width):
-            cols = slice(first, first + width)
-            nc.vector.tensor_tensor(
-                page_of(n)[:].indirect(idx2[:, first // 16 : (first + width) // 16]),
-                h[:, cols],
-                put_weight[:, cols],
-                ALU.mult,
-            )
+            return pages[0]
 
         def read(n, x, first, width):
             cols = slice(first, first + width)
@@ -170,7 +161,6 @@ def tile_list_refill_urgency_scores_kernel(
                 ALU.mult,
             )
 
-        hs = {}
         weighed = {}
 
         def products(n, half):
@@ -201,19 +191,23 @@ def tile_list_refill_urgency_scores_kernel(
                 )
             return need, less
 
-        def features_fused(n, half):
-            b, i = divmod(n, PACK)
-            cols = slice(half * BANK, (half + 1) * BANK)
-            if half == 0:
-                hs[n] = ring.tile([P, S], F32, name="h", tag="weighed", bufs=3)
-            need, less = products(n, half)
-            gate = ring.tile([P, BANK], F32, name="gate", tag="gate_half", bufs=2)
-            nc.scalar.activation(gate[:], need[:], ACT.Sigmoid)
-            nc.vector.scalar_tensor_tensor(
-                hs[n][:, cols], gate[:], gains[:, b, i : i + 1], less[:], ALU.mult, ALU.subtract
-            )
+        def features_first():
+            weighed[0] = ring.tile([P, S], F32, name="weighed", tag="weighed")
+            for half in range(2):
+                cols = slice(half * BANK, (half + 1) * BANK)
+                need, less = products(0, half)
+                gate = ring.tile([P, BANK], F32, name="gate", tag="gate_half", bufs=2)
+                nc.scalar.activation(gate[:], need[:], ACT.Sigmoid)
+                nc.vector.scalar_tensor_tensor(
+                    weighed[0][:, cols], gate[:], gains[:, 0, 0:1], less[:], ALU.mult, ALU.subtract
+                )
+            for half in range(2):
+                cols = slice(half * BANK, (half + 1) * BANK)
+                nc.vector.tensor_tensor(weighed[0][:, cols], weighed[0][:, cols], put_weight[:, cols], ALU.mult)
 
-        def features(n):
+        terms = {}
+
+        def features(n, parts=1):
             b, i = divmod(n, PACK)
             gate = ring.tile([P, S], F32, name="gate", tag="gate")
             linear = ring.tile([P, S], F32, name="linear", tag="linear")
@@ -222,11 +216,20 @@ def tile_list_refill_urgency_scores_kernel(
                 need, less = products(n, half)
                 nc.scalar.activation(gate[:, cols], need[:], ACT.Sigmoid)
                 nc.scalar.copy(linear[:, cols], less[:])
-            nc.scalar.activation(gate[:], gate[:], ACT.Copy, scale=gains[:, b, i : i + 1])
-            h = ring.tile([P, S], F32, name="h", tag="hx%d" % (n % 2), bufs=1)
-            nc.gpsimd.tensor_tensor(h[:], gate[:], linear[:], ALU.subtract)
-            weighed[n] = ring.tile([P, S], F32, name="weighed", tag="weighed", bufs=3)
-            nc.gpsimd.tensor_tensor(weighed[n][:], h[:], put_weight[:], ALU.mult)
+                if parts == 2:
+                    nc.scalar.activation(gate[:, cols], gate[:, cols], ACT.Copy, scale=gains[:, b, i : i + 1])
+            if parts == 1:
+                nc.scalar.activation(gate[:], gate[:], ACT.Copy, scale=gains[:, b, i : i + 1])
+            terms[n] = (gate, linear)
+
+        def weigh(n, parts=1):
+            gate, linear = terms[n]
+            h = ring.tile([P, S], F32, name="h", tag="turn%d" % (n % 2), bufs=1)
+            weighed[n] = ring.tile([P, S], F32, name="weighed", tag="weighed")
+            for part in range(parts):
+                cols = slice(part * S // parts, (part + 1) * S // parts)
+                nc.gpsimd.tensor_tensor(h[:, cols], gate[:, cols], linear[:, cols], ALU.subtract)
+                nc.gpsimd.tensor_tensor(weighed[n][:, cols], h[:, cols], put_weight[:, cols], ALU.mult)
 
         def put_weighed(n):
             nc.vector.tensor_copy(page_of(n)[:].indirect(idx2[:]), weighed[n][:])
@@ -242,30 +245,44 @@ def tile_list_refill_urgency_scores_kernel(
                     stop=(pos == len(tiles) - 1),
                 )
 
-        z_turned = {}
+        z_terms = {}
+        SPLIT = 512
 
         def stock_rows(n):
             b, i = divmod(n, PACK)
             return stocks[b][:, i * M : (i + 1) * M]
 
-        def excess(n, picked, parts):
-            over = ring.tile([P, M], F32, name="over", tag="hx%d" % ((n + 1) % 2), bufs=1)
-            width = M // parts
-            for part in range(parts):
-                cols = slice(part * width, (part + 1) * width)
-                nc.gpsimd.tensor_tensor(over[:, cols], picked[:, cols], read_weight[:, cols], ALU.mult)
-                nc.gpsimd.tensor_tensor(over[:, cols], over[:, cols], stock_rows(n)[:, cols], ALU.subtract)
-                nc.scalar.activation(over[:, cols], over[:, cols], ACT.Relu, scale=2.0)
-            return over
+        def gather(n, target, first, width, weight):
+            nc.vector.tensor_tensor(
+                target,
+                page_of(n)[:].indirect(idx3[:, first // 16 : (first + width) // 16]),
+                weight[:, first : first + width],
+                ALU.mult,
+            )
 
-        def turn_z(n, over):
-            turned = ring.tile([P, M], F32, name="z_turned", tag="z_turned", bufs=3)
-            for half in range(M // BANK):
+        def turn(tiles, width, func, scale, tag):
+            turned = ring.tile([P, width], F32, name=tag, tag=tag, bufs=3)
+            for first in range(0, width, BANK):
+                part = min(BANK, width - first)
                 bank = psum.tile([P, BANK], F32, name="bank", tag="work", bufs=4)
-                for block in range(BANK // P):
-                    add_turned(bank, block, [stock_rows(n), over], half * BANK + block * P)
-                nc.scalar.copy(turned[:, half * BANK : (half + 1) * BANK], bank[:])
-            z_turned[n] = turned
+                for block in range(part // P):
+                    add_turned(bank, block, tiles, first + block * P)
+                nc.scalar.activation(turned[:, first : first + part], bank[:, 0:part], func, scale=scale)
+            return turned
+
+        def read_slice(n, split):
+            near = ring.tile([P, split], F32, name="near", tag="turn%d" % (n % 2), bufs=1)
+            gather(n, near[:], 0, split, minus_weight)
+            far = None
+            if split < M:
+                far = ring.tile([P, M - split], F32, name="far", tag="far")
+                gather(n, far[:], split, M - split, minus_weight)
+            return near, far
+
+        def excess_near(n, near, first, width, over):
+            cols = slice(first, first + width)
+            nc.gpsimd.tensor_tensor(over[:, cols], near[:, cols], stock_rows(n)[:, cols], ALU.add)
+            nc.scalar.activation(over[:, cols], over[:, cols], ACT.Relu, scale=-2.0)
 
         z_bf = {}
 
@@ -280,18 +297,27 @@ def tile_list_refill_urgency_scores_kernel(
                 bank = psum.tile([P, BANK], F32, name="bank", tag="work", bufs=4)
                 for side in range(2):
                     for block in range(CHUNK // P):
-                        add_turned(bank, side * (CHUNK // P) + block, [z_turned[n + side]], c * CHUNK + block * P)
+                        col = c * CHUNK + block * P
+                        whole, parts = z_terms[n + side]
+                        if col < SPLIT:
+                            add_turned(bank, side * (CHUNK // P) + block, [whole], col)
+                        else:
+                            add_turned(bank, side * (CHUNK // P) + block, parts, col - SPLIT)
                 nc.scalar.copy(z_tile(b, c)[:, :, i : i + 2], bank[:].rearrange("p (s m) -> p m s", s=2))
 
         z_codes = [keep.tile([P, M], U32, name="z_codes%d" % b, align_bytes=64) for b in range(r_passes)]
         z_plane = [keep.tile([P, M], U8, name="z_plane%d" % b, align_bytes=64) for b in range(r_passes)]
 
-        def quantise_z(b, c):
-            cols = slice(c * CHUNK, (c + 1) * CHUNK)
+        def z_part(b, first, width):
+            c, low = divmod(first, CHUNK)
+            return z_tile(b, c)[:, low : low + width, :]
+
+        def quantise_z(b, first, width):
+            cols = slice(first, first + width)
             nc.vector.quantize_mx(
                 out=z_codes[b][:, cols].bitcast(FP8X4),
                 scales=z_plane[b][:, cols],
-                in_=z_tile(b, c)[:].rearrange("p m i -> p (m i)"),
+                in_=z_part(b, first, width).rearrange("p m i -> p (m i)"),
             )
 
         w3_codes = keep.tile([P, r_passes * N], U32, name="w3_codes", align_bytes=64)
@@ -314,100 +340,119 @@ def tile_list_refill_urgency_scores_kernel(
 
         score_banks = {}
 
-        def score_pass(c, b):
-            cols = slice(c * CHUNK, (c + 1) * CHUNK)
+        def score_pass(piece, b, tags):
+            first, width = piece
+            cols = slice(first, first + width)
+            per_bank = BANK // width
             if b == 0:
-                score_banks[c] = [
-                    psum.tile([P, BANK], F32, name="pair_bank", tag="need"),
-                    psum.tile([P, BANK], F32, name="lone_bank", tag="less"),
+                score_banks[piece] = [
+                    psum.tile([P, BANK], F32, name="score", tag=tag, bufs=(4 if tag == "work" else 2)) for tag in tags
                 ]
-            for tile_n in range(N // P):
-                first = b * N + tile_n * P
+            tiles = N // P
+            for tile_n in range(tiles):
+                lhs = b * N + tile_n * P
+                place = tile_n % per_bank
                 nc.tensor.matmul_mx(
-                    out=score_banks[c][tile_n // 2][:, (tile_n % 2) * CHUNK : (tile_n % 2 + 1) * CHUNK],
-                    lhsT=w3_codes[:, first : first + P].bitcast(FP8X4),
-                    lhsT_scale=w3_plane[:, first : first + P],
+                    out=score_banks[piece][tile_n // per_bank][:, place * width : (place + 1) * width],
+                    lhsT=w3_codes[:, lhs : lhs + P].bitcast(FP8X4),
+                    lhsT_scale=w3_plane[:, lhs : lhs + P],
                     rhs=z_codes[b][:, cols].bitcast(FP8X4),
                     rhs_scale=z_plane[b][:, cols],
-                    start=(b == 0 and tile_n != 1),
-                    stop=(b == r_passes - 1 and tile_n != 0),
+                    start=(b == 0 and place == 0),
+                    stop=(b == r_passes - 1 and (place == per_bank - 1 or tile_n == tiles - 1)),
                 )
 
-        def store_scores(c, lone_copy):
-            cols = slice(c * CHUNK, (c + 1) * CHUNK)
-            pair = ring.tile([P, BANK], F32, name="staged_pair", tag="staged_pair", bufs=3)
-            nc.scalar.copy(pair[:], score_banks[c][0][:])
-            nc.sync.dma_start(
-                out[0 : 2 * P, cols].rearrange("(g p) m -> p g m", p=P), pair[:].rearrange("p (g m) -> p g m", m=CHUNK)
-            )
-            lone = ring.tile([P, CHUNK], F32, name="staged_lone", tag="staged_lone", bufs=3)
-            lone_copy(lone[:], score_banks[c][1][:, 0:CHUNK])
-            nc.sync.dma_start(out[2 * P : N, cols], lone[:])
+        def store_scores(piece, copies):
+            first, width = piece
+            per_bank = BANK // width
+            tiles = N // P
+            for bank, low, copy in zip(score_banks[piece], range(0, tiles, per_bank), copies):
+                count = min(per_bank, tiles - low)
+                staged = ring.tile([P, count * width], F32, name="staged", tag="staged", bufs=8)
+                copy(staged[:], bank[:, 0 : count * width])
+                nc.sync.dma_start(
+                    out[low * P : (low + count) * P, first : first + width].rearrange("(g p) m -> p g m", p=P),
+                    staged[:].rearrange("p (g m) -> p g m", m=width),
+                )
 
-        stocks = [load_stock(0)]
         for a in range(k_passes):
             w1_raw[1, a] = load_rows(w1, a, slice(PASS, 2 * PASS), "w1_1%d" % a)
-        stocks.append(load_stock(1))
-        for half in range(2):
-            features_fused(0, half)
-            put(0, hs[0], half * BANK, BANK)
-        for half in range(2):
-            features_fused(1, half)
+        stocks = [load_stock(0)]
+        features_first()
+        put_weighed(0)
+        features(1, 2)
+        weigh(1, 2)
+        minus_weight = read_weight
+        nc.scalar.mul(minus_weight[:], read_weight[:], -1.0)
         features(2)
         pair_in = keep.tile([P, 2, M], F32, name="pair_in")
         for n in range(last):
-            picked = ring.tile([P, M], F32, name="picked", tag="picked")
-            nc.vector.tensor_copy(picked[:], page_of(n)[:].indirect(idx3[:]))
-            if n == 0:
-                put(1, hs[1], 0, S)
-                for a in range(k_passes):
-                    quantise_w1(1, a, [(0, PACK, nc.scalar.copy)])
-            else:
-                put_weighed(n + 1)
-            if n + 3 < slices and False:
-                features(n + 3)
-            over = excess(n, picked, 2 if n == last - 1 else 1)
-            if n + 3 < slices and True:
-                features(n + 3)
+            split = M if n == last - 1 else SPLIT
+            near, far = read_slice(n, split)
+            put_weighed(n + 1)
+            over = ring.tile([P, split], F32, name="over", tag="turn%d" % ((n + 1) % 2), bufs=1)
             if n == last - 1:
-                for half in range(M // BANK):
+                for half in range(2):
+                    excess_near(n, near, half * BANK, BANK, over)
+                for half in range(2):
                     cols = slice(half * BANK, (half + 1) * BANK)
                     nc.gpsimd.tensor_tensor(pair_in[:, 0, cols], over[:, cols], stock_rows(n)[:, cols], ALU.add)
             else:
-                turn_z(n, over)
+                excess_near(n, near, 0, split, over)
+                whole = turn([stock_rows(n), over], split, ACT.Copy, 1.0, "z_turned")
+            if n + 2 < slices:
+                weigh(n + 2)
+            if n == 0:
+                for a in range(k_passes):
+                    quantise_w1(1, a, [(0, PACK, nc.scalar.copy)])
+            if n + 3 < slices:
+                features(n + 3)
+            if n < last - 1:
+                rows = stock_rows(n)
+                parts = None
+                if split < M:
+                    parts = [
+                        turn([rows[:, split:M]], M - split, ACT.Copy, 1.0, "stock_turned"),
+                        turn([rows[:, split:M], far], M - split, ACT.Relu, -2.0, "excess_turned"),
+                    ]
+                z_terms[n] = (whole, parts)
             if n % 2 == 1:
                 z_pair(n - 1)
             if n == PACK - 1:
                 for c in range(M // CHUNK):
-                    quantise_z(0, c)
-            if n == 2:
+                    quantise_z(0, c * CHUNK, CHUNK)
+            if n == 0:
                 quantise_w3()
+                stocks.append(load_stock(1))
 
-        x_last = ring.tile([P, M], F32, name="x_last", tag="picked")
+        x_last = ring.tile([P, M], F32, name="x_last", tag="weighed")
         pair_stock = stocks[1][:, 2 * M : 4 * M].rearrange("p (s m) -> p m s", s=2)
-        chunks = M // CHUNK
-        score_pass(0, 0)
-        score_pass(1, 0)
-        for step in range(chunks + 3):
-            if step < chunks:
-                read(last, x_last, step * CHUNK, CHUNK)
-            if 1 <= step <= chunks:
-                cols = slice((step - 1) * CHUNK, step * CHUNK)
+        pair_view = pair_in[:].rearrange("p s m -> p m s")
+        pieces = [(0, 256), (256, 256), (512, 256), (768, 128), (896, 128)]
+        tags = [("need", "less"), ("need", "less"), ("work", "work"), ("work",), ("work",)]
+        direct = 2
+        for piece, tag in zip(pieces, tags):
+            score_pass(piece, 0, tag)
+        for step in range(len(pieces) + 3):
+            if step < len(pieces):
+                read(last, x_last, *pieces[step])
+            if 1 <= step <= len(pieces):
+                first, width = pieces[step - 1]
+                cols = slice(first, first + width)
                 nc.vector.scalar_tensor_tensor(
-                    pair_in[:, 1, cols], x_last[:, cols], 2.0, stock_rows(last)[:, cols], ALU.mult, ALU.subtract
+                    pair_in[:, 1, cols], x_last[:, cols], -2.0, stock_rows(last)[:, cols], ALU.mult, ALU.subtract
                 )
-            if 2 <= step <= chunks + 1:
-                c = step - 2
-                cols = slice(c * CHUNK, (c + 1) * CHUNK)
-                nc.vector.tensor_tensor(
-                    z_tile(1, c)[:, :, 2:4],
-                    pair_in[:].rearrange("p s m -> p m s")[:, cols, :],
-                    pair_stock[:, cols, :],
-                    ALU.max,
-                )
+            if 2 <= step <= len(pieces) + 1:
+                first, width = pieces[step - 2]
+                cols = slice(first, first + width)
+                target = z_part(1, first, width)[:, :, 2:4]
+                if step - 2 >= direct:
+                    nc.vector.tensor_tensor(target, pair_view[:, cols, :], pair_stock[:, cols, :], ALU.max)
+                else:
+                    nc.vector.tensor_tensor(pair_in[:, 1, cols], pair_in[:, 1, cols], stock_rows(last)[:, cols], ALU.max)
+                    nc.scalar.copy(target, pair_view[:, cols, :])
             if step >= 3:
-                quantise_z(1, step - 3)
-                score_pass(step - 3, 1)
-                store_scores(step - 3, nc.vector.tensor_copy if step == chunks + 2 else nc.scalar.copy)
-                if step - 1 < chunks:
-                    score_pass(step - 1, 0)
+                piece = pieces[step - 3]
+                quantise_z(1, *piece)
+                score_pass(piece, 1, None)
+                store_scores(piece, [nc.vector.tensor_copy if step - 3 == 4 else nc.scalar.copy, nc.vector.tensor_copy if step - 3 == 2 else nc.scalar.copy])

@@ -21,17 +21,29 @@ P = 128
 PACK = 4
 PASS = P * PACK
 BANK = 512
-CHUNK = 256
-QUADS = 4
+GROUP = 16
+QUAD = 32
+ROWS = 4
+SPREAD = 8
+ALIGN = 64
+K_PASSES = K // PASS
+R_PASSES = H // PASS
+SLICES = R_PASSES * PACK
+LAST = SLICES - 1
+HALVES = S // BANK
+CHUNK = BANK // 2
+N_TILES = N // P
+NEAR = M // 2
+WORK_BANKS = 4
+
+PIECES = [(0, CHUNK), (CHUNK, CHUNK), (2 * CHUNK, CHUNK), (3 * CHUNK, P), (3 * CHUNK + P, P)]
+PIECE_BANKS = [("need", "less"), ("need", "less"), ("work", "work"), ("work",), ("work",)]
 
 
 def tile_list_refill_urgency_scores_kernel(
     tc, tab_words, tab_scales, offs, offs2, offs3, w1, w2_words, w2_scales, gain, wgs, wgt, stock, w3, out
 ):
     nc = tc.nc
-    k_passes = K // PASS
-    r_passes = H // PASS
-    slices = r_passes * PACK
 
     with ExitStack() as ctx:
         lists = ctx.enter_context(tc.tile_pool(name="lists", bufs=1))
@@ -39,200 +51,201 @@ def tile_list_refill_urgency_scores_kernel(
         ring = ctx.enter_context(tc.tile_pool(name="ring", bufs=2))
         psum = ctx.enter_context(tc.psum_pool(name="psum", bufs=2))
 
-        idx = lists.tile([P, S // 16], U16, name="idx")
-        idx2 = lists.tile([P, S // 16], U16, name="idx2")
-        idx3 = lists.tile([P, M // 16], U16, name="idx3")
+        idx = lists.tile([P, S // GROUP], U16, name="idx")
+        idx2 = lists.tile([P, S // GROUP], U16, name="idx2")
+        idx3 = lists.tile([P, M // GROUP], U16, name="idx3")
 
-        tab_plane = keep.tile([P, T], U8, name="tab_plane", align_bytes=64)
-        nc.vector.memset(tab_plane[:].bitcast(I32), 0)
-        w2_plane_raw = keep.tile([P, k_passes * H], U8, name="w2_plane_raw", align_bytes=64)
-        nc.vector.memset(w2_plane_raw[:].bitcast(I32), 0)
-        v_plane1 = keep.tile([P, S], U8, name="v_plane1", align_bytes=64)
-        nc.vector.memset(v_plane1[:].bitcast(I32), 0)
-        pages = [keep.tile([P, T2], F32, name="page%d" % n) for n in range(1)]
-        for page in pages:
-            nc.vector.memset(page[:], 0.0)
+        def entries(offsets, first, width):
+            return offsets[:, first // GROUP : (first + width) // GROUP]
+
+        def work_bank():
+            return psum.tile([P, BANK], F32, name="work", tag="work", bufs=WORK_BANKS)
+
+        w2_scale_rows = keep.tile([P, K_PASSES * H], U8, name="w2_scale_rows", align_bytes=ALIGN)
+        nc.vector.memset(w2_scale_rows[:].bitcast(I32), 0)
+        tab_scale_rows = keep.tile([P, K_PASSES * T], U8, name="tab_scale_rows", align_bytes=ALIGN)
+        nc.vector.memset(tab_scale_rows[:].bitcast(I32), 0)
+        planes = keep.tile([P, K_PASSES * (S + H)], U8, name="planes", align_bytes=ALIGN)
+        nc.vector.memset(planes[:].bitcast(I32), 0)
+        page = keep.tile([P, T2], F32, name="page")
+        nc.vector.memset(page[:], 0.0)
         ident = keep.tile([P, P], F32, name="ident")
         make_identity(nc, ident[:])
-        warm = keep.tile([P, 2], F32, name="warm")
-        nc.vector.memset(warm[:, 0:1], 0.0)
 
         def load_table(a):
-            words = ring.tile([P, T], I32, name="tab%d" % a, tag="big", align_bytes=64)
+            words = ring.tile([P, T], I32, name="tab%d" % a, tag="big", align_bytes=ALIGN)
             nc.sync.dma_start(words[:], tab_words[a].rearrange("p t i -> p (t i)").bitcast(I32))
             return words
 
-        def load_rows(weight, a, cols, name):
-            width = cols.stop - cols.start
-            raw = ring.tile([P, PACK, width], F32, name=name, tag="raw")
-            nc.sync.dma_start(raw[:], weight[a * PASS : (a + 1) * PASS, cols].rearrange("(p i) c -> p i c", i=PACK))
+        def load_rows(weight, a, cols):
+            raw = ring.tile([P, PACK, cols.stop - cols.start], F32, name="raw", tag="raw")
+            nc.sync.dma_start(raw[:], weight[a * PASS : (a + 1) * PASS, cols].rearrange("(p j) c -> p j c", j=PACK))
             return raw
 
+        stocks = []
+
         def load_stock(b):
-            rows = ring.tile([P, PACK * M], F32, name="stock%d" % b, tag="big", align_bytes=64)
+            rows = ring.tile([P, PACK * M], F32, name="stock%d" % b, tag="big", align_bytes=ALIGN)
             nc.sync.dma_start(rows[:], stock[b * PASS : (b + 1) * PASS, :].rearrange("(p i) m -> p (i m)", i=PACK))
-            return rows
+            stocks.append(rows)
+
+        def stock_rows(n):
+            b, i = divmod(n, PACK)
+            return stocks[b][:, i * M : (i + 1) * M]
 
         nc.sync.dma_start(idx[:], offs)
-        w2_raw = keep.tile([P, k_passes, H // 2], I32, name="w2_raw")
+        w2_raw = keep.tile([P, K_PASSES, H // 2], I32, name="w2_raw")
         nc.sync.dma_start(w2_raw[:], w2_words.bitcast(I32).rearrange("a p c -> p a c"))
-        for q in range(QUADS):
+
+        def load_scale_rows(rows, scales):
             nc.sync.dma_start(
-                tab_plane[32 * q : 32 * q + 8, :].bitcast(I32), tab_scales[:, 4 * q : 4 * q + 4, :].bitcast(I32)
+                rows[0:P:SPREAD, :].bitcast(I32).rearrange("u (a c) -> u a c", a=K_PASSES),
+                scales.bitcast(I32).rearrange("a u c -> u a c"),
             )
+
+        load_scale_rows(w2_scale_rows, w2_scales)
+        gains = keep.tile([P, R_PASSES, PACK], F32, name="gains")
+        nc.sync.dma_start(gains[:], gain.rearrange("(b p i) -> p b i", b=R_PASSES, i=PACK))
+        nc.sync.dma_start(idx2[:], offs2)
+        load_scale_rows(tab_scale_rows, tab_scales)
         tab = [load_table(0)]
-        nc.scalar.activation(warm[:, 1:2], warm[:, 0:1], ACT.Sigmoid)
-        for q in range(QUADS):
-            nc.sync.dma_start(
-                w2_plane_raw[32 * q : 32 * q + 4, :].bitcast(I32).rearrange("r (a c) -> r a c", a=k_passes),
-                w2_scales[:, 4 * q : 4 * q + 4, :].bitcast(I32).rearrange("a r c -> r a c"),
+        w1_raw = {(0, a): load_rows(w1, a, slice(0, PASS)) for a in range(K_PASSES)}
+        tab.append(load_table(1))
+
+        def deal(target, source):
+            nc.vector.tensor_copy(
+                target.rearrange("p (g i q) -> p g i q", i=PACK, q=P),
+                source.rearrange("p (g q i) -> p g i q", i=PACK, q=P),
             )
-        w1_raw = {(0, a): load_rows(w1, a, slice(0, PASS), "w1_0%d" % a) for a in range(k_passes)}
-        w2_codes = keep.tile([P, k_passes * H * 2], U8, name="w2_codes", align_bytes=64)
-        nc.vector.tensor_copy(
-            w2_codes[:].bitcast(U16).rearrange("p (g i q) -> p g i q", i=PACK, q=P),
-            w2_raw[:].rearrange("p a c -> p (a c)").bitcast(U16).rearrange("p (g q i) -> p g i q", i=PACK, q=P),
-        )
+
+        v_scale_rows = keep.tile([P, K_PASSES * S], U8, name="v_scale_rows", tag="w2_codes", align_bytes=ALIGN)
+        all_rows = keep.tile([P, K_PASSES * (S + H)], U8, name="all_rows", align_bytes=ALIGN)
+        for a in range(K_PASSES):
+            window = tab_scale_rows[:, a * T : (a + 1) * T]
+            nc.vector.tensor_copy(v_scale_rows[:, a * S : (a + 1) * S], window.indirect(idx[:]))
+        deal(all_rows[:, K_PASSES * S :], w2_scale_rows[:])
+        nc.vector.tensor_copy(all_rows[:, 0 : K_PASSES * S].bitcast(I32), v_scale_rows[:].bitcast(I32))
+        for r in range(ROWS):
+            nc.sync.dma_start(planes[r:P:QUAD, :].bitcast(I32), all_rows[SPREAD * r : P : QUAD, :].bitcast(I32))
+        v_plane = [planes[:, a * S : (a + 1) * S] for a in range(K_PASSES)]
+        w2_plane = planes[:, K_PASSES * S :]
+        w2_codes = keep.tile([P, K_PASSES * H * 2], U8, name="w2_codes", tag="w2_codes", align_bytes=ALIGN)
+        deal(w2_codes[:].bitcast(U16), w2_raw[:].rearrange("p a c -> p (a c)").bitcast(U16))
+
         v_words = [
-            [keep.tile([P, BANK], U32, name="v_words%d%d" % (a, half), align_bytes=64) for half in range(2)]
-            for a in range(k_passes)
+            [keep.tile([P, BANK], U32, name="v_words%d%d" % (a, half), align_bytes=ALIGN) for half in range(HALVES)]
+            for a in range(K_PASSES)
         ]
-        v_plane = keep.tile([P, S], U8, name="v_plane", align_bytes=64)
 
         def gather_words(a):
-            for half in range(2):
-                nc.vector.tensor_copy(
-                    v_words[a][half][:], tab[a][:].bitcast(U32).indirect(idx[:, half * 32 : (half + 1) * 32])
-                )
+            for half in range(HALVES):
+                window = tab[a][:].bitcast(U32)
+                nc.vector.tensor_copy(v_words[a][half][:], window.indirect(entries(idx, half * BANK, BANK)))
 
-        nc.vector.tensor_copy(v_plane[:], tab_plane[:].indirect(idx[:]))
         gather_words(0)
-        tab.append(load_table(1))
-        nc.scalar.dma_start(v_plane1[0 : P - 4, :].bitcast(I32), v_plane[4:P, :].bitcast(I32))
-        gains = keep.tile([P, r_passes, PACK], F32, name="gains")
-        nc.sync.dma_start(gains[:], gain.rearrange("(b p i) -> p b i", b=r_passes, i=PACK))
-        nc.sync.dma_start(idx2[:], offs2)
+        nc.sync.dma_start(idx3[:], offs3)
         put_weight = keep.tile([P, S], F32, name="put_weight")
         nc.sync.dma_start(put_weight[:], wgs)
-        nc.sync.dma_start(idx3[:], offs3)
-        read_weight = keep.tile([P, M], F32, name="read_weight")
-        nc.sync.dma_start(read_weight[:], wgt)
-
-        w2_plane = keep.tile([P, k_passes * H], U8, name="w2_plane", align_bytes=64)
-        nc.vector.tensor_copy(
-            w2_plane[:].rearrange("p (g i q) -> p g i q", i=PACK, q=P),
-            w2_plane_raw[:].rearrange("p (g q i) -> p g i q", i=PACK, q=P),
-        )
+        minus_wgt = keep.tile([P, M], F32, name="minus_wgt")
+        nc.sync.dma_start(minus_wgt[:], wgt)
 
         w1_codes = {}
         w1_plane = {}
 
-        def quantise_w1(b, a, parts):
-            codes = keep.tile([P, PASS], U32, name="w1_codes%d%d" % (b, a), align_bytes=64)
-            plane = keep.tile([P, PASS], U8, name="w1_plane%d%d" % (b, a), align_bytes=64)
-            w1_codes[b, a], w1_plane[b, a] = codes, plane
-            rounded = []
-            for first, count, copy in parts:
-                part = ring.tile([P, count * PASS], BF16, name="w1_bf", tag="w1_bf", bufs=2, align_bytes=64)
-                copy(
-                    part[:].rearrange("p (i q j) -> p q i j", i=count, j=PACK),
-                    w1_raw[b, a][:].rearrange("p j (q i) -> p q i j", i=PACK)[:, :, first : first + count, :],
-                )
-                rounded.append(part)
-            for (first, count, copy), part in zip(parts, rounded):
-                cols = slice(first * P, (first + count) * P)
-                nc.vector.quantize_mx(out=codes[:, cols].bitcast(FP8X4), scales=plane[:, cols], in_=part[:])
-
-        for a in range(k_passes):
-            quantise_w1(0, a, [(0, PACK, nc.scalar.copy)])
-        gather_words(1)
-
-        last = slices - 1
-
-        def page_of(n):
-            return pages[0]
-
-        def read(n, x, first, width):
-            cols = slice(first, first + width)
-            nc.vector.tensor_tensor(
-                x[:, cols],
-                page_of(n)[:].indirect(idx3[:, first // 16 : (first + width) // 16]),
-                read_weight[:, cols],
-                ALU.mult,
+        def quantise_w1(b, a):
+            rounded = ring.tile([P, PACK * PASS], BF16, name="w1_bf", tag="w1_bf", align_bytes=ALIGN)
+            nc.scalar.copy(
+                rounded[:].rearrange("p (i q j) -> p q i j", i=PACK, j=PACK),
+                w1_raw[b, a][:].rearrange("p j (q i) -> p q i j", i=PACK),
             )
+            w1_codes[b, a] = keep.tile([P, PASS], U32, name="w1_codes%d%d" % (b, a), align_bytes=ALIGN)
+            w1_plane[b, a] = keep.tile([P, PASS], U8, name="w1_plane%d%d" % (b, a), align_bytes=ALIGN)
+            nc.vector.quantize_mx(out=w1_codes[b, a][:].bitcast(FP8X4), scales=w1_plane[b, a][:], in_=rounded[:])
 
-        weighed = {}
+        for a in range(K_PASSES):
+            quantise_w1(0, a)
+        gather_words(1)
 
         def products(n, half):
             b, i = divmod(n, PACK)
             cols = slice(half * BANK, (half + 1) * BANK)
             need = psum.tile([P, BANK], F32, name="need", tag="need")
             less = psum.tile([P, BANK], F32, name="less", tag="less")
-            for a in range(k_passes):
+            for a in range(K_PASSES):
                 nc.tensor.matmul_mx(
                     out=need[:],
                     lhsT=w1_codes[b, a][:, i * P : (i + 1) * P].bitcast(FP8X4),
                     lhsT_scale=w1_plane[b, a][:, i * P : (i + 1) * P],
                     rhs=v_words[a][half][:].bitcast(FP8X4),
-                    rhs_scale=v_plane[4 * a : P, cols],
+                    rhs_scale=v_plane[a][:, cols],
                     start=(a == 0),
-                    stop=(a == k_passes - 1),
+                    stop=(a == K_PASSES - 1),
                 )
-            for a in range(k_passes):
+            for a in range(K_PASSES):
                 first = a * H + n * P
                 nc.tensor.matmul_mx(
                     out=less[:],
                     lhsT=w2_codes[:, 2 * first : 2 * (first + P)].bitcast(FP4X4),
                     lhsT_scale=w2_plane[:, first : first + P],
                     rhs=v_words[a][half][:].bitcast(FP8X4),
-                    rhs_scale=[v_plane, v_plane1][a][:, cols],
+                    rhs_scale=v_plane[a][:, cols],
                     start=(a == 0),
-                    stop=(a == k_passes - 1),
+                    stop=(a == K_PASSES - 1),
                 )
             return need, less
 
-        def features_first():
+        def cuts(parts):
+            return [slice(part * S // parts, (part + 1) * S // parts) for part in range(parts)]
+
+        weighed = {}
+        terms = {}
+
+        def weigh_first():
             weighed[0] = ring.tile([P, S], F32, name="weighed", tag="weighed")
-            for half in range(2):
-                cols = slice(half * BANK, (half + 1) * BANK)
+            for half, cols in enumerate(cuts(HALVES)):
                 need, less = products(0, half)
-                gate = ring.tile([P, BANK], F32, name="gate", tag="gate_half", bufs=2)
+                gate = ring.tile([P, BANK], F32, name="gate_first", tag="gate_first")
                 nc.scalar.activation(gate[:], need[:], ACT.Sigmoid)
                 nc.vector.scalar_tensor_tensor(
                     weighed[0][:, cols], gate[:], gains[:, 0, 0:1], less[:], ALU.mult, ALU.subtract
                 )
-            for half in range(2):
-                cols = slice(half * BANK, (half + 1) * BANK)
+            for cols in cuts(HALVES):
                 nc.vector.tensor_tensor(weighed[0][:, cols], weighed[0][:, cols], put_weight[:, cols], ALU.mult)
 
-        terms = {}
-
-        def features(n, parts=1):
+        def features(n, parts):
             b, i = divmod(n, PACK)
             gate = ring.tile([P, S], F32, name="gate", tag="gate")
             linear = ring.tile([P, S], F32, name="linear", tag="linear")
-            for half in range(2):
-                cols = slice(half * BANK, (half + 1) * BANK)
+            for half, cols in enumerate(cuts(HALVES)):
                 need, less = products(n, half)
                 nc.scalar.activation(gate[:, cols], need[:], ACT.Sigmoid)
                 nc.scalar.copy(linear[:, cols], less[:])
-                if parts == 2:
-                    nc.scalar.activation(gate[:, cols], gate[:, cols], ACT.Copy, scale=gains[:, b, i : i + 1])
-            if parts == 1:
-                nc.scalar.activation(gate[:], gate[:], ACT.Copy, scale=gains[:, b, i : i + 1])
+                for done in cuts(parts):
+                    if done.stop == cols.stop:
+                        nc.scalar.activation(gate[:, done], gate[:, done], ACT.Copy, scale=gains[:, b, i : i + 1])
             terms[n] = (gate, linear)
 
-        def weigh(n, parts=1):
+        def chain_tile(name, width, parity):
+            return ring.tile([P, width], F32, name=name, tag="chain%d" % (parity % 2), bufs=1)
+
+        def weigh(n, parts):
             gate, linear = terms[n]
-            h = ring.tile([P, S], F32, name="h", tag="turn%d" % (n % 2), bufs=1)
+            h = chain_tile("h", S, n)
             weighed[n] = ring.tile([P, S], F32, name="weighed", tag="weighed")
-            for part in range(parts):
-                cols = slice(part * S // parts, (part + 1) * S // parts)
+            for cols in cuts(parts):
                 nc.gpsimd.tensor_tensor(h[:, cols], gate[:, cols], linear[:, cols], ALU.subtract)
                 nc.gpsimd.tensor_tensor(weighed[n][:, cols], h[:, cols], put_weight[:, cols], ALU.mult)
 
-        def put_weighed(n):
-            nc.vector.tensor_copy(page_of(n)[:].indirect(idx2[:]), weighed[n][:])
+        def put(n):
+            nc.vector.tensor_copy(page[:].indirect(idx2[:]), weighed[n][:])
+
+        def read(minus_x, first, width):
+            window = page[:].indirect(entries(idx3, first, width))
+            nc.vector.tensor_tensor(minus_x, window, minus_wgt[:, first : first + width], ALU.mult)
+
+        def excess_near(n, minus_x, excess, cols):
+            nc.gpsimd.tensor_tensor(excess[:, cols], minus_x[:, cols], stock_rows(n)[:, cols], ALU.add)
+            nc.scalar.activation(excess[:, cols], excess[:, cols], ACT.Relu, scale=-2.0)
 
         def add_turned(bank, block, tiles, col):
             for pos, source in enumerate(tiles):
@@ -245,72 +258,36 @@ def tile_list_refill_urgency_scores_kernel(
                     stop=(pos == len(tiles) - 1),
                 )
 
-        z_terms = {}
-        SPLIT = 512
-
-        def stock_rows(n):
-            b, i = divmod(n, PACK)
-            return stocks[b][:, i * M : (i + 1) * M]
-
-        def gather(n, target, first, width, weight):
-            nc.vector.tensor_tensor(
-                target,
-                page_of(n)[:].indirect(idx3[:, first // 16 : (first + width) // 16]),
-                weight[:, first : first + width],
-                ALU.mult,
-            )
-
-        def turn(tiles, width, func, scale, tag):
-            turned = ring.tile([P, width], F32, name=tag, tag=tag, bufs=3)
-            for first in range(0, width, BANK):
-                part = min(BANK, width - first)
-                bank = psum.tile([P, BANK], F32, name="bank", tag="work", bufs=4)
-                for block in range(part // P):
-                    add_turned(bank, block, tiles, first + block * P)
-                nc.scalar.activation(turned[:, first : first + part], bank[:, 0:part], func, scale=scale)
+        def turn(tiles, func, scale, tag):
+            turned = ring.tile([P, BANK], F32, name=tag, tag=tag, bufs=3)
+            bank = work_bank()
+            for block in range(BANK // P):
+                add_turned(bank, block, tiles, block * P)
+            nc.scalar.activation(turned[:], bank[:], func, scale=scale)
             return turned
 
-        def read_slice(n, split):
-            near = ring.tile([P, split], F32, name="near", tag="turn%d" % (n % 2), bufs=1)
-            gather(n, near[:], 0, split, minus_weight)
-            far = None
-            if split < M:
-                far = ring.tile([P, M - split], F32, name="far", tag="far")
-                gather(n, far[:], split, M - split, minus_weight)
-            return near, far
-
-        def excess_near(n, near, first, width, over):
-            cols = slice(first, first + width)
-            nc.gpsimd.tensor_tensor(over[:, cols], near[:, cols], stock_rows(n)[:, cols], ALU.add)
-            nc.scalar.activation(over[:, cols], over[:, cols], ACT.Relu, scale=-2.0)
-
+        z_terms = {}
         z_bf = {}
-
-        def z_tile(b, c):
-            if (b, c) not in z_bf:
-                z_bf[b, c] = ring.tile([P, CHUNK, PACK], BF16, name="z_bf", tag="z_bf", bufs=4, align_bytes=64)
-            return z_bf[b, c]
-
-        def z_pair(n):
-            b, i = divmod(n, PACK)
-            for c in range(M // CHUNK):
-                bank = psum.tile([P, BANK], F32, name="bank", tag="work", bufs=4)
-                for side in range(2):
-                    for block in range(CHUNK // P):
-                        col = c * CHUNK + block * P
-                        whole, parts = z_terms[n + side]
-                        if col < SPLIT:
-                            add_turned(bank, side * (CHUNK // P) + block, [whole], col)
-                        else:
-                            add_turned(bank, side * (CHUNK // P) + block, parts, col - SPLIT)
-                nc.scalar.copy(z_tile(b, c)[:, :, i : i + 2], bank[:].rearrange("p (s m) -> p m s", s=2))
-
-        z_codes = [keep.tile([P, M], U32, name="z_codes%d" % b, align_bytes=64) for b in range(r_passes)]
-        z_plane = [keep.tile([P, M], U8, name="z_plane%d" % b, align_bytes=64) for b in range(r_passes)]
 
         def z_part(b, first, width):
             c, low = divmod(first, CHUNK)
-            return z_tile(b, c)[:, low : low + width, :]
+            if (b, c) not in z_bf:
+                shape = [P, CHUNK, PACK]
+                z_bf[b, c] = ring.tile(shape, BF16, name="z_bf", tag="z_bf", bufs=M // CHUNK, align_bytes=ALIGN)
+            return z_bf[b, c][:, low : low + width, :]
+
+        def z_pair(n):
+            b, i = divmod(n, PACK)
+            for first in range(0, M, CHUNK):
+                bank = work_bank()
+                for side in range(2):
+                    for block in range(CHUNK // P):
+                        part, col = divmod(first + block * P, NEAR)
+                        add_turned(bank, side * (CHUNK // P) + block, z_terms[n + side][part], col)
+                nc.scalar.copy(z_part(b, first, CHUNK)[:, :, i : i + 2], bank[:].rearrange("p (s m) -> p m s", s=2))
+
+        z_codes = [keep.tile([P, M], U32, name="z_codes%d" % b, align_bytes=ALIGN) for b in range(R_PASSES)]
+        z_plane = [keep.tile([P, M], U8, name="z_plane%d" % b, align_bytes=ALIGN) for b in range(R_PASSES)]
 
         def quantise_z(b, first, width):
             cols = slice(first, first + width)
@@ -320,13 +297,13 @@ def tile_list_refill_urgency_scores_kernel(
                 in_=z_part(b, first, width).rearrange("p m i -> p (m i)"),
             )
 
-        w3_codes = keep.tile([P, r_passes * N], U32, name="w3_codes", align_bytes=64)
-        w3_plane = keep.tile([P, r_passes * N], U8, name="w3_plane", align_bytes=64)
+        w3_codes = keep.tile([P, R_PASSES * N], U32, name="w3_codes", align_bytes=ALIGN)
+        w3_plane = keep.tile([P, R_PASSES * N], U8, name="w3_plane", align_bytes=ALIGN)
 
         def quantise_w3():
-            rounded = keep.tile([P, r_passes * N * PACK], BF16, name="w3_bf", align_bytes=64)
-            for b in range(r_passes):
-                raw = load_rows(w3, b, slice(0, N), "w3_raw")
+            rounded = keep.tile([P, R_PASSES * N * PACK], BF16, name="w3_bf", align_bytes=ALIGN)
+            for b in range(R_PASSES):
+                raw = load_rows(w3, b, slice(0, N))
                 nc.scalar.copy(
                     rounded[:, b * N * PACK : (b + 1) * N * PACK].rearrange("p (c e j) -> p c j e", e=4, j=PACK),
                     raw[:].rearrange("p j (c e) -> p c j e", e=4),
@@ -340,16 +317,11 @@ def tile_list_refill_urgency_scores_kernel(
 
         score_banks = {}
 
-        def score_pass(piece, b, tags):
+        def score_pass(piece, b):
             first, width = piece
             cols = slice(first, first + width)
             per_bank = BANK // width
-            if b == 0:
-                score_banks[piece] = [
-                    psum.tile([P, BANK], F32, name="score", tag=tag, bufs=(4 if tag == "work" else 2)) for tag in tags
-                ]
-            tiles = N // P
-            for tile_n in range(tiles):
+            for tile_n in range(N_TILES):
                 lhs = b * N + tile_n * P
                 place = tile_n % per_bank
                 nc.tensor.matmul_mx(
@@ -359,15 +331,14 @@ def tile_list_refill_urgency_scores_kernel(
                     rhs=z_codes[b][:, cols].bitcast(FP8X4),
                     rhs_scale=z_plane[b][:, cols],
                     start=(b == 0 and place == 0),
-                    stop=(b == r_passes - 1 and (place == per_bank - 1 or tile_n == tiles - 1)),
+                    stop=(b == R_PASSES - 1 and (place == per_bank - 1 or tile_n == N_TILES - 1)),
                 )
 
         def store_scores(piece, copies):
             first, width = piece
             per_bank = BANK // width
-            tiles = N // P
-            for bank, low, copy in zip(score_banks[piece], range(0, tiles, per_bank), copies):
-                count = min(per_bank, tiles - low)
+            for bank, low, copy in zip(score_banks[piece], range(0, N_TILES, per_bank), copies):
+                count = min(per_bank, N_TILES - low)
                 staged = ring.tile([P, count * width], F32, name="staged", tag="staged", bufs=8)
                 copy(staged[:], bank[:, 0 : count * width])
                 nc.sync.dma_start(
@@ -375,84 +346,100 @@ def tile_list_refill_urgency_scores_kernel(
                     staged[:].rearrange("p (g m) -> p g m", m=width),
                 )
 
-        for a in range(k_passes):
-            w1_raw[1, a] = load_rows(w1, a, slice(PASS, 2 * PASS), "w1_1%d" % a)
-        stocks = [load_stock(0)]
-        features_first()
-        put_weighed(0)
-        features(1, 2)
-        weigh(1, 2)
-        minus_weight = read_weight
-        nc.scalar.mul(minus_weight[:], read_weight[:], -1.0)
-        features(2)
+        for a in range(K_PASSES):
+            w1_raw[1, a] = load_rows(w1, a, slice(PASS, 2 * PASS))
+        load_stock(0)
+        weigh_first()
+        put(0)
+        features(1, HALVES)
+        weigh(1, HALVES)
+        nc.scalar.mul(minus_wgt[:], minus_wgt[:], -1.0)
+        features(2, 1)
         pair_in = keep.tile([P, 2, M], F32, name="pair_in")
-        for n in range(last):
-            split = M if n == last - 1 else SPLIT
-            near, far = read_slice(n, split)
-            put_weighed(n + 1)
-            over = ring.tile([P, split], F32, name="over", tag="turn%d" % ((n + 1) % 2), bufs=1)
-            if n == last - 1:
-                for half in range(2):
-                    excess_near(n, near, half * BANK, BANK, over)
-                for half in range(2):
-                    cols = slice(half * BANK, (half + 1) * BANK)
-                    nc.gpsimd.tensor_tensor(pair_in[:, 0, cols], over[:, cols], stock_rows(n)[:, cols], ALU.add)
-            else:
-                excess_near(n, near, 0, split, over)
-                whole = turn([stock_rows(n), over], split, ACT.Copy, 1.0, "z_turned")
-            if n + 2 < slices:
-                weigh(n + 2)
+        for n in range(LAST - 1):
+            far = ring.tile([P, M - NEAR], F32, name="far", tag="far")
+            read(far[:], NEAR, M - NEAR)
+            near = chain_tile("near", NEAR, n)
+            read(near[:], 0, NEAR)
+            put(n + 1)
+            excess = chain_tile("excess", NEAR, n + 1)
+            excess_near(n, near, excess, slice(0, NEAR))
+            z_near = turn([stock_rows(n), excess], ACT.Copy, 1.0, "z_turned")
+            weigh(n + 2, 1)
             if n == 0:
-                for a in range(k_passes):
-                    quantise_w1(1, a, [(0, PACK, nc.scalar.copy)])
-            if n + 3 < slices:
-                features(n + 3)
-            if n < last - 1:
-                rows = stock_rows(n)
-                parts = None
-                if split < M:
-                    parts = [
-                        turn([rows[:, split:M]], M - split, ACT.Copy, 1.0, "stock_turned"),
-                        turn([rows[:, split:M], far], M - split, ACT.Relu, -2.0, "excess_turned"),
-                    ]
-                z_terms[n] = (whole, parts)
+                for a in range(K_PASSES):
+                    quantise_w1(1, a)
+            if n + 3 < SLICES:
+                features(n + 3, 1)
+            stock_far = stock_rows(n)[:, NEAR:M]
+            z_terms[n] = (
+                [z_near],
+                [
+                    turn([stock_far], ACT.Copy, 1.0, "stock_turned"),
+                    turn([stock_far, far], ACT.Relu, -2.0, "excess_turned"),
+                ],
+            )
             if n % 2 == 1:
                 z_pair(n - 1)
             if n == PACK - 1:
-                for c in range(M // CHUNK):
-                    quantise_z(0, c * CHUNK, CHUNK)
+                for first in range(0, M, CHUNK):
+                    quantise_z(0, first, CHUNK)
             if n == 0:
                 quantise_w3()
-                stocks.append(load_stock(1))
+                load_stock(1)
 
-        x_last = ring.tile([P, M], F32, name="x_last", tag="weighed")
-        pair_stock = stocks[1][:, 2 * M : 4 * M].rearrange("p (s m) -> p m s", s=2)
+        n = LAST - 1
+        near = chain_tile("near", M, n)
+        read(near[:], 0, M)
+        put(LAST)
+        excess = chain_tile("excess", M, n + 1)
+        for cols in cuts(HALVES):
+            excess_near(n, near, excess, cols)
+        for cols in cuts(HALVES):
+            nc.gpsimd.tensor_tensor(pair_in[:, 0, cols], excess[:, cols], stock_rows(n)[:, cols], ALU.add)
+
+        minus_x = ring.tile([P, M], F32, name="minus_x_last", tag="weighed")
         pair_view = pair_in[:].rearrange("p s m -> p m s")
-        pieces = [(0, 256), (256, 256), (512, 256), (768, 128), (896, 128)]
-        tags = [("need", "less"), ("need", "less"), ("work", "work"), ("work",), ("work",)]
-        direct = 2
-        for piece, tag in zip(pieces, tags):
-            score_pass(piece, 0, tag)
-        for step in range(len(pieces) + 3):
-            if step < len(pieces):
-                read(last, x_last, *pieces[step])
-            if 1 <= step <= len(pieces):
-                first, width = pieces[step - 1]
-                cols = slice(first, first + width)
-                nc.vector.scalar_tensor_tensor(
-                    pair_in[:, 1, cols], x_last[:, cols], -2.0, stock_rows(last)[:, cols], ALU.mult, ALU.subtract
-                )
-            if 2 <= step <= len(pieces) + 1:
-                first, width = pieces[step - 2]
-                cols = slice(first, first + width)
-                target = z_part(1, first, width)[:, :, 2:4]
-                if step - 2 >= direct:
-                    nc.vector.tensor_tensor(target, pair_view[:, cols, :], pair_stock[:, cols, :], ALU.max)
-                else:
-                    nc.vector.tensor_tensor(pair_in[:, 1, cols], pair_in[:, 1, cols], stock_rows(last)[:, cols], ALU.max)
-                    nc.scalar.copy(target, pair_view[:, cols, :])
-            if step >= 3:
-                piece = pieces[step - 3]
-                quantise_z(1, *piece)
-                score_pass(piece, 1, None)
-                store_scores(piece, [nc.vector.tensor_copy if step - 3 == 4 else nc.scalar.copy, nc.vector.tensor_copy if step - 3 == 2 else nc.scalar.copy])
+        pair_stock = stocks[1][:, 2 * M : 4 * M].rearrange("p (s m) -> p m s", s=2)
+        for piece, tags in zip(PIECES, PIECE_BANKS):
+            score_banks[piece] = [
+                work_bank() if tag == "work" else psum.tile([P, BANK], F32, name="score", tag=tag) for tag in tags
+            ]
+            score_pass(piece, 0)
+
+        def twice_x_less_stock(first, width):
+            cols = slice(first, first + width)
+            nc.vector.scalar_tensor_tensor(
+                pair_in[:, 1, cols], minus_x[:, cols], -2.0, stock_rows(LAST)[:, cols], ALU.mult, ALU.subtract
+            )
+
+        def round_last_pair(first, width):
+            cols = slice(first, first + width)
+            target = z_part(1, first, width)[:, :, 2:4]
+            if width == CHUNK:
+                nc.vector.tensor_tensor(pair_in[:, 1, cols], pair_in[:, 1, cols], stock_rows(LAST)[:, cols], ALU.max)
+                nc.scalar.copy(target, pair_view[:, cols, :])
+            else:
+                nc.vector.tensor_tensor(target, pair_view[:, cols, :], pair_stock[:, cols, :], ALU.max)
+
+        def finish(first, width):
+            piece = (first, width)
+            quantise_z(1, first, width)
+            score_pass(piece, 1)
+            last_wide = first + width == 3 * CHUNK
+            store_scores(
+                piece,
+                [
+                    nc.vector.tensor_copy if piece == PIECES[-1] else nc.scalar.copy,
+                    nc.vector.tensor_copy if last_wide else nc.scalar.copy,
+                ],
+            )
+
+        def read_last(first, width):
+            read(minus_x[:, first : first + width], first, width)
+
+        stages = [read_last, twice_x_less_stock, round_last_pair, finish]
+        for step in range(len(PIECES) + len(stages) - 1):
+            for lag, stage in enumerate(stages):
+                if 0 <= step - lag < len(PIECES):
+                    stage(*PIECES[step - lag])

from contextlib import ExitStack

import concourse.mybir as mybir
from concourse.masks import make_identity

K, T, S, H, T2, M, N = 1024, 4096, 1024, 1024, 2048, 1024, 384
FLOPS = 2 * (2 * K * H * S + H * N * M)

F32 = mybir.dt.float32
BF16 = mybir.dt.bfloat16
I32 = mybir.dt.int32
U32 = mybir.dt.uint32
U16 = mybir.dt.uint16
U8 = mybir.dt.uint8
FP8X4 = mybir.dt.float8_e4m3fn_x4
FP4X4 = mybir.dt.float4_e2m1fn_x4
ALU = mybir.AluOpType
ACT = mybir.ActivationFunctionType

P = 128
PACK = 4
PASS = P * PACK
BANK = 512
GROUP = 16
QUAD = 32
ROWS = 4
SPREAD = 8
ALIGN = 64
K_PASSES = K // PASS
R_PASSES = H // PASS
SLICES = R_PASSES * PACK
LAST = SLICES - 1
HALVES = S // BANK
CHUNK = BANK // 2
N_TILES = N // P
NEAR = M // 2
WORK_BANKS = 4

PIECES = [(0, CHUNK), (CHUNK, CHUNK), (2 * CHUNK, CHUNK), (3 * CHUNK, P), (3 * CHUNK + P, P)]
PIECE_BANKS = [("need", "less"), ("need", "less"), ("work", "work"), ("work",), ("work",)]


def tile_list_refill_urgency_scores_kernel(
    tc, tab_words, tab_scales, offs, offs2, offs3, w1, w2_words, w2_scales, gain, wgs, wgt, stock, w3, out
):
    nc = tc.nc

    with ExitStack() as ctx:
        lists = ctx.enter_context(tc.tile_pool(name="lists", bufs=1))
        keep = ctx.enter_context(tc.tile_pool(name="keep", bufs=1))
        ring = ctx.enter_context(tc.tile_pool(name="ring", bufs=2))
        psum = ctx.enter_context(tc.psum_pool(name="psum", bufs=2))

        idx = lists.tile([P, S // GROUP], U16, name="idx")
        idx2 = lists.tile([P, S // GROUP], U16, name="idx2")
        idx3 = lists.tile([P, M // GROUP], U16, name="idx3")

        def entries(offsets, first, width):
            return offsets[:, first // GROUP : (first + width) // GROUP]

        def work_bank():
            return psum.tile([P, BANK], F32, name="work", tag="work", bufs=WORK_BANKS)

        w2_scale_rows = keep.tile([P, K_PASSES * H], U8, name="w2_scale_rows", align_bytes=ALIGN)
        nc.vector.memset(w2_scale_rows[:].bitcast(I32), 0)
        tab_scale_rows = keep.tile([P, K_PASSES * T], U8, name="tab_scale_rows", align_bytes=ALIGN)
        nc.vector.memset(tab_scale_rows[:].bitcast(I32), 0)
        planes = keep.tile([P, K_PASSES * (S + H)], U8, name="planes", align_bytes=ALIGN)
        nc.vector.memset(planes[:].bitcast(I32), 0)
        page = keep.tile([P, T2], F32, name="page")
        nc.vector.memset(page[:], 0.0)
        ident = keep.tile([P, P], F32, name="ident")
        make_identity(nc, ident[:])

        def load_table(a):
            words = ring.tile([P, T], I32, name="tab%d" % a, tag="big", align_bytes=ALIGN)
            nc.sync.dma_start(words[:], tab_words[a].rearrange("p t i -> p (t i)").bitcast(I32))
            return words

        def load_rows(weight, a, cols):
            raw = ring.tile([P, PACK, cols.stop - cols.start], F32, name="raw", tag="raw")
            nc.sync.dma_start(raw[:], weight[a * PASS : (a + 1) * PASS, cols].rearrange("(p j) c -> p j c", j=PACK))
            return raw

        stocks = []

        def load_stock(b):
            rows = ring.tile([P, PACK * M], F32, name="stock%d" % b, tag="big", align_bytes=ALIGN)
            nc.sync.dma_start(rows[:], stock[b * PASS : (b + 1) * PASS, :].rearrange("(p i) m -> p (i m)", i=PACK))
            stocks.append(rows)

        def stock_rows(n):
            b, i = divmod(n, PACK)
            return stocks[b][:, i * M : (i + 1) * M]

        nc.sync.dma_start(idx[:], offs)
        w2_raw = keep.tile([P, K_PASSES, H // 2], I32, name="w2_raw")
        nc.sync.dma_start(w2_raw[:], w2_words.bitcast(I32).rearrange("a p c -> p a c"))

        def load_scale_rows(rows, scales):
            nc.sync.dma_start(
                rows[0:P:SPREAD, :].bitcast(I32).rearrange("u (a c) -> u a c", a=K_PASSES),
                scales.bitcast(I32).rearrange("a u c -> u a c"),
            )

        load_scale_rows(w2_scale_rows, w2_scales)
        gains = keep.tile([P, R_PASSES, PACK], F32, name="gains")
        nc.sync.dma_start(gains[:], gain.rearrange("(b p i) -> p b i", b=R_PASSES, i=PACK))
        nc.sync.dma_start(idx2[:], offs2)
        load_scale_rows(tab_scale_rows, tab_scales)
        tab = [load_table(0)]
        w1_raw = {(0, a): load_rows(w1, a, slice(0, PASS)) for a in range(K_PASSES)}
        tab.append(load_table(1))

        def deal(target, source):
            nc.vector.tensor_copy(
                target.rearrange("p (g i q) -> p g i q", i=PACK, q=P),
                source.rearrange("p (g q i) -> p g i q", i=PACK, q=P),
            )

        v_scale_rows = keep.tile([P, K_PASSES * S], U8, name="v_scale_rows", tag="w2_codes", align_bytes=ALIGN)
        all_rows = keep.tile([P, K_PASSES * (S + H)], U8, name="all_rows", align_bytes=ALIGN)
        for a in range(K_PASSES):
            window = tab_scale_rows[:, a * T : (a + 1) * T]
            nc.vector.tensor_copy(v_scale_rows[:, a * S : (a + 1) * S], window.indirect(idx[:]))
        deal(all_rows[:, K_PASSES * S :], w2_scale_rows[:])
        nc.vector.tensor_copy(all_rows[:, 0 : K_PASSES * S].bitcast(I32), v_scale_rows[:].bitcast(I32))
        for r in range(ROWS):
            nc.sync.dma_start(planes[r:P:QUAD, :].bitcast(I32), all_rows[SPREAD * r : P : QUAD, :].bitcast(I32))
        v_plane = [planes[:, a * S : (a + 1) * S] for a in range(K_PASSES)]
        w2_plane = planes[:, K_PASSES * S :]
        w2_codes = keep.tile([P, K_PASSES * H * 2], U8, name="w2_codes", tag="w2_codes", align_bytes=ALIGN)
        deal(w2_codes[:].bitcast(U16), w2_raw[:].rearrange("p a c -> p (a c)").bitcast(U16))

        v_words = [
            [keep.tile([P, BANK], U32, name="v_words%d%d" % (a, half), align_bytes=ALIGN) for half in range(HALVES)]
            for a in range(K_PASSES)
        ]

        def gather_words(a):
            for half in range(HALVES):
                window = tab[a][:].bitcast(U32)
                nc.vector.tensor_copy(v_words[a][half][:], window.indirect(entries(idx, half * BANK, BANK)))

        gather_words(0)
        nc.sync.dma_start(idx3[:], offs3)
        put_weight = keep.tile([P, S], F32, name="put_weight")
        nc.sync.dma_start(put_weight[:], wgs)
        minus_wgt = keep.tile([P, M], F32, name="minus_wgt")
        nc.sync.dma_start(minus_wgt[:], wgt)

        w1_codes = {}
        w1_plane = {}

        def quantise_w1(b, a):
            rounded = ring.tile([P, PACK * PASS], BF16, name="w1_bf", tag="w1_bf", align_bytes=ALIGN)
            nc.scalar.copy(
                rounded[:].rearrange("p (i q j) -> p q i j", i=PACK, j=PACK),
                w1_raw[b, a][:].rearrange("p j (q i) -> p q i j", i=PACK),
            )
            w1_codes[b, a] = keep.tile([P, PASS], U32, name="w1_codes%d%d" % (b, a), align_bytes=ALIGN)
            w1_plane[b, a] = keep.tile([P, PASS], U8, name="w1_plane%d%d" % (b, a), align_bytes=ALIGN)
            nc.vector.quantize_mx(out=w1_codes[b, a][:].bitcast(FP8X4), scales=w1_plane[b, a][:], in_=rounded[:])

        for a in range(K_PASSES):
            quantise_w1(0, a)
        gather_words(1)

        def products(n, half):
            b, i = divmod(n, PACK)
            cols = slice(half * BANK, (half + 1) * BANK)
            need = psum.tile([P, BANK], F32, name="need", tag="need")
            less = psum.tile([P, BANK], F32, name="less", tag="less")
            for a in range(K_PASSES):
                nc.tensor.matmul_mx(
                    out=need[:],
                    lhsT=w1_codes[b, a][:, i * P : (i + 1) * P].bitcast(FP8X4),
                    lhsT_scale=w1_plane[b, a][:, i * P : (i + 1) * P],
                    rhs=v_words[a][half][:].bitcast(FP8X4),
                    rhs_scale=v_plane[a][:, cols],
                    start=(a == 0),
                    stop=(a == K_PASSES - 1),
                )
            for a in range(K_PASSES):
                first = a * H + n * P
                nc.tensor.matmul_mx(
                    out=less[:],
                    lhsT=w2_codes[:, 2 * first : 2 * (first + P)].bitcast(FP4X4),
                    lhsT_scale=w2_plane[:, first : first + P],
                    rhs=v_words[a][half][:].bitcast(FP8X4),
                    rhs_scale=v_plane[a][:, cols],
                    start=(a == 0),
                    stop=(a == K_PASSES - 1),
                )
            return need, less

        def cuts(parts):
            return [slice(part * S // parts, (part + 1) * S // parts) for part in range(parts)]

        weighed = {}
        terms = {}

        def weigh_first():
            weighed[0] = ring.tile([P, S], F32, name="weighed", tag="weighed")
            for half, cols in enumerate(cuts(HALVES)):
                need, less = products(0, half)
                gate = ring.tile([P, BANK], F32, name="gate_first", tag="gate_first")
                nc.scalar.activation(gate[:], need[:], ACT.Sigmoid)
                nc.vector.scalar_tensor_tensor(
                    weighed[0][:, cols], gate[:], gains[:, 0, 0:1], less[:], ALU.mult, ALU.subtract
                )
            for cols in cuts(HALVES):
                nc.vector.tensor_tensor(weighed[0][:, cols], weighed[0][:, cols], put_weight[:, cols], ALU.mult)

        def features(n, parts):
            b, i = divmod(n, PACK)
            gate = ring.tile([P, S], F32, name="gate", tag="gate")
            linear = ring.tile([P, S], F32, name="linear", tag="linear")
            for half, cols in enumerate(cuts(HALVES)):
                need, less = products(n, half)
                nc.scalar.activation(gate[:, cols], need[:], ACT.Sigmoid)
                nc.scalar.copy(linear[:, cols], less[:])
                for done in cuts(parts):
                    if done.stop == cols.stop:
                        nc.scalar.activation(gate[:, done], gate[:, done], ACT.Copy, scale=gains[:, b, i : i + 1])
            terms[n] = (gate, linear)

        def chain_tile(name, width, parity):
            return ring.tile([P, width], F32, name=name, tag="chain%d" % (parity % 2), bufs=1)

        def weigh(n, parts):
            gate, linear = terms[n]
            h = chain_tile("h", S, n)
            weighed[n] = ring.tile([P, S], F32, name="weighed", tag="weighed")
            for cols in cuts(parts):
                nc.gpsimd.tensor_tensor(h[:, cols], gate[:, cols], linear[:, cols], ALU.subtract)
                nc.gpsimd.tensor_tensor(weighed[n][:, cols], h[:, cols], put_weight[:, cols], ALU.mult)

        def put(n):
            nc.vector.tensor_copy(page[:].indirect(idx2[:]), weighed[n][:])

        def read(minus_x, first, width):
            window = page[:].indirect(entries(idx3, first, width))
            nc.vector.tensor_tensor(minus_x, window, minus_wgt[:, first : first + width], ALU.mult)

        def excess_near(n, minus_x, excess, cols):
            nc.gpsimd.tensor_tensor(excess[:, cols], minus_x[:, cols], stock_rows(n)[:, cols], ALU.add)
            nc.scalar.activation(excess[:, cols], excess[:, cols], ACT.Relu, scale=-2.0)

        def add_turned(bank, block, tiles, col):
            for pos, source in enumerate(tiles):
                nc.tensor.matmul(
                    bank[:, block * P : (block + 1) * P],
                    lhsT=source[:, col : col + P],
                    rhs=ident[:],
                    is_transpose=True,
                    start=(pos == 0),
                    stop=(pos == len(tiles) - 1),
                )

        def turn(tiles, func, scale, tag):
            turned = ring.tile([P, BANK], F32, name=tag, tag=tag, bufs=3)
            bank = work_bank()
            for block in range(BANK // P):
                add_turned(bank, block, tiles, block * P)
            nc.scalar.activation(turned[:], bank[:], func, scale=scale)
            return turned

        z_terms = {}
        z_bf = {}

        def z_part(b, first, width):
            c, low = divmod(first, CHUNK)
            if (b, c) not in z_bf:
                shape = [P, CHUNK, PACK]
                z_bf[b, c] = ring.tile(shape, BF16, name="z_bf", tag="z_bf", bufs=M // CHUNK, align_bytes=ALIGN)
            return z_bf[b, c][:, low : low + width, :]

        def z_pair(n):
            b, i = divmod(n, PACK)
            for first in range(0, M, CHUNK):
                bank = work_bank()
                for side in range(2):
                    for block in range(CHUNK // P):
                        part, col = divmod(first + block * P, NEAR)
                        add_turned(bank, side * (CHUNK // P) + block, z_terms[n + side][part], col)
                nc.scalar.copy(z_part(b, first, CHUNK)[:, :, i : i + 2], bank[:].rearrange("p (s m) -> p m s", s=2))

        z_codes = [keep.tile([P, M], U32, name="z_codes%d" % b, align_bytes=ALIGN) for b in range(R_PASSES)]
        z_plane = [keep.tile([P, M], U8, name="z_plane%d" % b, align_bytes=ALIGN) for b in range(R_PASSES)]

        def quantise_z(b, first, width):
            cols = slice(first, first + width)
            nc.vector.quantize_mx(
                out=z_codes[b][:, cols].bitcast(FP8X4),
                scales=z_plane[b][:, cols],
                in_=z_part(b, first, width).rearrange("p m i -> p (m i)"),
            )

        w3_codes = keep.tile([P, R_PASSES * N], U32, name="w3_codes", align_bytes=ALIGN)
        w3_plane = keep.tile([P, R_PASSES * N], U8, name="w3_plane", align_bytes=ALIGN)

        def quantise_w3():
            rounded = keep.tile([P, R_PASSES * N * PACK], BF16, name="w3_bf", align_bytes=ALIGN)
            for b in range(R_PASSES):
                raw = load_rows(w3, b, slice(0, N))
                nc.scalar.copy(
                    rounded[:, b * N * PACK : (b + 1) * N * PACK].rearrange("p (c e j) -> p c j e", e=4, j=PACK),
                    raw[:].rearrange("p j (c e) -> p c j e", e=4),
                )
            for first, width in ((0, 512), (512, 256)):
                nc.vector.quantize_mx(
                    out=w3_codes[:, first : first + width].bitcast(FP8X4),
                    scales=w3_plane[:, first : first + width],
                    in_=rounded[:, first * PACK : (first + width) * PACK],
                )

        score_banks = {}

        def score_pass(piece, b):
            first, width = piece
            cols = slice(first, first + width)
            per_bank = BANK // width
            for tile_n in range(N_TILES):
                lhs = b * N + tile_n * P
                place = tile_n % per_bank
                nc.tensor.matmul_mx(
                    out=score_banks[piece][tile_n // per_bank][:, place * width : (place + 1) * width],
                    lhsT=w3_codes[:, lhs : lhs + P].bitcast(FP8X4),
                    lhsT_scale=w3_plane[:, lhs : lhs + P],
                    rhs=z_codes[b][:, cols].bitcast(FP8X4),
                    rhs_scale=z_plane[b][:, cols],
                    start=(b == 0 and place == 0),
                    stop=(b == R_PASSES - 1 and (place == per_bank - 1 or tile_n == N_TILES - 1)),
                )

        def store_scores(piece, copies):
            first, width = piece
            per_bank = BANK // width
            for bank, low, copy in zip(score_banks[piece], range(0, N_TILES, per_bank), copies):
                count = min(per_bank, N_TILES - low)
                staged = ring.tile([P, count * width], F32, name="staged", tag="staged", bufs=8)
                copy(staged[:], bank[:, 0 : count * width])
                nc.sync.dma_start(
                    out[low * P : (low + count) * P, first : first + width].rearrange("(g p) m -> p g m", p=P),
                    staged[:].rearrange("p (g m) -> p g m", m=width),
                )

        for a in range(K_PASSES):
            w1_raw[1, a] = load_rows(w1, a, slice(PASS, 2 * PASS))
        load_stock(0)
        weigh_first()
        put(0)
        features(1, HALVES)
        weigh(1, HALVES)
        nc.scalar.mul(minus_wgt[:], minus_wgt[:], -1.0)
        features(2, 1)
        pair_in = keep.tile([P, 2, M], F32, name="pair_in")
        for n in range(LAST - 1):
            far = ring.tile([P, M - NEAR], F32, name="far", tag="far")
            read(far[:], NEAR, M - NEAR)
            near = chain_tile("near", NEAR, n)
            read(near[:], 0, NEAR)
            put(n + 1)
            excess = chain_tile("excess", NEAR, n + 1)
            excess_near(n, near, excess, slice(0, NEAR))
            z_near = turn([stock_rows(n), excess], ACT.Copy, 1.0, "z_turned")
            weigh(n + 2, 1)
            if n == 0:
                for a in range(K_PASSES):
                    quantise_w1(1, a)
            if n + 3 < SLICES:
                features(n + 3, 1)
            stock_far = stock_rows(n)[:, NEAR:M]
            z_terms[n] = (
                [z_near],
                [
                    turn([stock_far], ACT.Copy, 1.0, "stock_turned"),
                    turn([stock_far, far], ACT.Relu, -2.0, "excess_turned"),
                ],
            )
            if n % 2 == 1:
                z_pair(n - 1)
            if n == PACK - 1:
                for first in range(0, M, CHUNK):
                    quantise_z(0, first, CHUNK)
            if n == 0:
                quantise_w3()
                load_stock(1)

        n = LAST - 1
        near = chain_tile("near", M, n)
        read(near[:], 0, M)
        put(LAST)
        excess = chain_tile("excess", M, n + 1)
        for cols in cuts(HALVES):
            excess_near(n, near, excess, cols)
        for cols in cuts(HALVES):
            nc.gpsimd.tensor_tensor(pair_in[:, 0, cols], excess[:, cols], stock_rows(n)[:, cols], ALU.add)

        minus_x = ring.tile([P, M], F32, name="minus_x_last", tag="weighed")
        pair_view = pair_in[:].rearrange("p s m -> p m s")
        pair_stock = stocks[1][:, 2 * M : 4 * M].rearrange("p (s m) -> p m s", s=2)
        for piece, tags in zip(PIECES, PIECE_BANKS):
            score_banks[piece] = [
                work_bank() if tag == "work" else psum.tile([P, BANK], F32, name="score", tag=tag) for tag in tags
            ]
            score_pass(piece, 0)

        def twice_x_less_stock(first, width):
            cols = slice(first, first + width)
            nc.vector.scalar_tensor_tensor(
                pair_in[:, 1, cols], minus_x[:, cols], -2.0, stock_rows(LAST)[:, cols], ALU.mult, ALU.subtract
            )

        def round_last_pair(first, width):
            cols = slice(first, first + width)
            target = z_part(1, first, width)[:, :, 2:4]
            if width == CHUNK:
                nc.vector.tensor_tensor(pair_in[:, 1, cols], pair_in[:, 1, cols], stock_rows(LAST)[:, cols], ALU.max)
                nc.scalar.copy(target, pair_view[:, cols, :])
            else:
                nc.vector.tensor_tensor(target, pair_view[:, cols, :], pair_stock[:, cols, :], ALU.max)

        def finish(first, width):
            piece = (first, width)
            quantise_z(1, first, width)
            score_pass(piece, 1)
            last_wide = first + width == 3 * CHUNK
            store_scores(
                piece,
                [
                    nc.vector.tensor_copy if piece == PIECES[-1] else nc.scalar.copy,
                    nc.vector.tensor_copy if last_wide else nc.scalar.copy,
                ],
            )

        def read_last(first, width):
            read(minus_x[:, first : first + width], first, width)

        stages = [read_last, twice_x_less_stock, round_last_pair, finish]
        for step in range(len(PIECES) + len(stages) - 1):
            for lag, stage in enumerate(stages):
                if 0 <= step - lag < len(PIECES):
                    stage(*PIECES[step - lag])
